import numpy as np
import ml_dtypes


def mxq(x, axis, fmt="e4m3"):
    dtype, down = {"e4m3": (ml_dtypes.float8_e4m3fn, 7), "e5m2": (ml_dtypes.float8_e5m2, 14)}[fmt]
    v = np.moveaxis(np.asarray(x, np.float32).astype(ml_dtypes.bfloat16).astype(np.float64), axis, -1)
    blocks = v.reshape(v.shape[:-1] + (-1, 32))
    amax = np.abs(blocks).max(-1, keepdims=True)
    byte = np.maximum(np.where(amax > 0, np.frexp(amax)[1] - 1 + 127, 0) - down, 1)
    scale = np.exp2(byte - 127.0)
    codes = (blocks / scale).astype(np.float32).astype(dtype).astype(np.float64)
    return np.moveaxis((codes * scale).reshape(v.shape), -1, axis)


WIDE = False


def mx_kscale(k):
    if not WIDE:
        return np.ones(k)
    levels = np.array([10, -10, 5, -5, 0])
    if k % 512:
        return np.exp2(np.random.permutation(np.resize(levels, k // 32))).repeat(32)
    a = np.empty((k // 512, 16))
    for p in range(k // 512):
        a[p, :8] = np.random.permutation(np.resize(levels, 8))
        for g in range(8):
            far = levels[np.abs(levels - a[p, g]) >= 10]
            a[p, g + 8] = far[np.random.randint(len(far))]
    return np.exp2(a.ravel()).repeat(32)


def f64(x):
    return np.asarray(x).astype(np.float64)


def striped(idx):
    return np.tile(idx.reshape(-1, 16).T, (8, 1)).astype(np.uint16)


def unstriped(offs):
    return offs[:16].T.reshape(-1).astype(np.int64)


E2M1 = np.array([0.0, 0.5, 1.0, 1.5, 2.0, 3.0, 4.0, 6.0, -0.0, -0.5, -1.0, -1.5, -2.0, -3.0, -4.0, -6.0])


def pack_weight(w, fmt):
    k, n = w.shape
    w = f64(np.asarray(w, np.float32).astype(ml_dtypes.bfloat16)).reshape(k // 32, 32, n)
    amax = np.abs(w).max(1)
    if fmt == "e4m3":
        byte = np.frexp(amax)[1] - 1 + 127 - 7
    else:
        mant, ex = np.frexp(amax / 6.0)
        byte = np.where(mant > 0.5, ex, ex - 1) + 127
    byte = np.clip(np.where(amax > 0, byte, 1), 1, 254)
    scaled = (w * np.exp2(127.0 - byte)[:, None, :]).reshape(k, n).astype(np.float32)
    by_word = np.ascontiguousarray(scaled.reshape(k // 512, 128, 4, n).transpose(0, 1, 3, 2))
    if fmt == "e4m3":
        words = by_word.astype(ml_dtypes.float8_e4m3fn).view(np.uint8)
    else:
        c = by_word.astype(ml_dtypes.float4_e2m1fn).view(np.uint8) & 0xF
        words = (c[..., 0::2] | (c[..., 1::2] << 4)).reshape(k // 512, 128, 2 * n)
    return np.ascontiguousarray(words), np.ascontiguousarray(byte.astype(np.uint8).reshape(k // 512, 16, n))


def unpack_weight(words, scales, fmt):
    g, _, n = scales.shape
    words = np.ascontiguousarray(words).reshape(g, 128, n, -1)
    if fmt == "e4m3":
        vals = words.view(ml_dtypes.float8_e4m3fn).astype(np.float64)
    else:
        nib = np.empty((g, 128, n, 4), np.uint8)
        nib[..., 0::2] = words & 0xF
        nib[..., 1::2] = words >> 4
        vals = E2M1[nib]
    vals = vals * np.repeat(np.exp2(scales.astype(np.float64) - 127.0), 8, axis=1)[..., None]
    return vals.transpose(0, 1, 3, 2).reshape(g * 512, n)


def gelu(v):
    return 0.5 * v * (1.0 + np.tanh(np.sqrt(2.0 / np.pi) * (v + 0.044715 * v**3)))


def bf(x):
    return np.asarray(x, np.float32).astype(ml_dtypes.bfloat16)


def planes(Y):
    n, m = Y.shape
    b = f64(bf(Y)).reshape(n // 32, 32, m)
    amax = np.abs(b).max(1)
    byte = np.clip(np.where(amax > 0, np.frexp(amax)[1] - 1 + 127 - 7, 1), 1, 254)
    codes = (b * np.exp2(127.0 - byte)[:, None, :]).reshape(n, m).astype(np.float32).astype(ml_dtypes.float8_e4m3fn).view(np.uint8)
    words = codes.reshape(n // 512, 128, 4, m).transpose(0, 1, 3, 2)
    return np.ascontiguousarray(words), np.ascontiguousarray(byte.astype(np.uint8).reshape(n // 512, 16, m))


K, K2, T, S, H, N, T2 = 512, 1024, 2048, 1024, 1024, 512, 2048

def setup_inputs():
    n = np.random.standard_normal
    s, s2, u = mx_kscale(K)[:, None], mx_kscale(K2)[:, None], mx_kscale(H)[:, None]
    size = np.exp(0.8 * n(N))
    tab_words, tab_scales = pack_weight(n((K, T)) * s, "e4m3")
    tab2_words, tab2_scales = pack_weight(n((K2, T)) * s2, "e4m3")
    w2_words, w2_scales = pack_weight(n((K, H)) / np.sqrt(K) / s, "e2m1")
    w3_words, w3_scales = pack_weight(n((K2, H)) / np.sqrt(K2) / s2, "e4m3")
    perm = np.random.permutation(T2)
    return {
        "tab_words": tab_words, "tab_scales": tab_scales,
        "tab2_words": tab2_words, "tab2_scales": tab2_scales,
        "offs": striped(np.random.permutation(T)[:S]),
        "offs2": striped(np.random.permutation(T)[:S]),
        "offs3": striped(perm[:S]), "offs4": striped(perm[S:]),
        "w1": (n((K, H)) / np.sqrt(K) / s).astype(np.float32),
        "w2_words": w2_words, "w2_scales": w2_scales,
        "w3_words": w3_words, "w3_scales": w3_scales,
        "wg1": np.exp(0.3 * n((128, S))).astype(np.float32),
        "wg2": np.exp(0.3 * n((128, S))).astype(np.float32),
        "gain": (np.exp(0.3 * n(H)) * u[:, 0]).astype(np.float32),
        "w4": (n((H, N)) / np.sqrt(H) / u * size[None, :]).astype(np.float32),
        "up": (n((N, T2)) * size[:, None]).astype(np.float32)}

def reference(tab_words, tab_scales, tab2_words, tab2_scales, offs, offs2, offs3, offs4, w1,
              w2_words, w2_scales, w3_words, w3_scales, wg1, wg2, gain, w4, up):
    v = unpack_weight(tab_words, tab_scales, "e4m3")[:, unstriped(offs)]
    v2 = unpack_weight(tab2_words, tab2_scales, "e4m3")[:, unstriped(offs2)]
    h1 = np.minimum(mxq(f64(w1), 0, "e4m3").T @ v,
                    unpack_weight(w2_words, w2_scales, "e2m1").T @ v)
    b = unpack_weight(w3_words, w3_scales, "e4m3").T @ v2
    h2 = b / np.sqrt(1.0 + np.square(b))
    page = np.zeros((H, T2))
    page[:, unstriped(offs3)] = np.tile(f64(wg1), (H // 128, 1)) * h1
    page[:, unstriped(offs4)] = np.tile(f64(wg2), (H // 128, 1)) * h2
    z = page * f64(gain)[:, None]
    y = f64(up) + (mxq(f64(w4), 0, "e4m3").T @ mxq(z, 0, "e4m3"))
    words, scales = planes(y)
    return y, words, scales

@@ -1,0 +1,346 @@
+from contextlib import ExitStack
+
+import concourse.mybir as mybir
+
+K, K2, T, S, H, N, T2 = 512, 1024, 2048, 1024, 1024, 512, 2048
+FLOPS = 2 * S * H * (2 * K + K2) + 2 * H * N * T2
+
+F32 = mybir.dt.float32
+BF16 = mybir.dt.bfloat16
+I32 = mybir.dt.int32
+U32 = mybir.dt.uint32
+U16 = mybir.dt.uint16
+U8 = mybir.dt.uint8
+FP8X4 = mybir.dt.float8_e4m3fn_x4
+FP4X4 = mybir.dt.float4_e2m1fn_x4
+ALU = mybir.AluOpType
+ACT = mybir.ActivationFunctionType
+
+P = 128
+PACK = 4
+BANK = 512
+ROW_TILES = H // P
+CHUNKS = T2 // BANK
+HYBRID = True
+
+
+def tile_list_woven_video_residual_kernel(
+    tc, tab_words, tab_scales, tab2_words, tab2_scales, offs, offs2, offs3, offs4, w1,
+    w2_words, w2_scales, w3_words, w3_scales, wg1, wg2, gain, w4, up, out_0, out_1, out_2,
+):
+    nc = tc.nc
+    with ExitStack() as ctx:
+        keep = ctx.enter_context(tc.tile_pool(name="keep", bufs=1))
+        big = ctx.enter_context(tc.tile_pool(name="big", bufs=6))
+        cast = ctx.enter_context(tc.tile_pool(name="cast", bufs=2))
+        pages = ctx.enter_context(tc.tile_pool(name="pages", bufs=3))
+        woven = ctx.enter_context(tc.tile_pool(name="woven", bufs=CHUNKS))
+        work = ctx.enter_context(tc.tile_pool(name="work", bufs=2))
+        psum = ctx.enter_context(tc.psum_pool(name="psum", bufs=8))
+
+        def kept(name, shape, dtype):
+            return keep.tile(shape, dtype, name=name, align_bytes=64)
+
+        def staged(name, shape, dtype):
+            return big.tile(shape, dtype, name=name, tag="big", align_bytes=64)
+
+        def new_bank(name):
+            return psum.tile([P, BANK], F32, name=name, tag="bank")
+
+        def load_list(name, src):
+            lst = keep.tile([P, S // 16], U16, name=name)
+            nc.sync.dma_start(lst[:], src)
+            return lst
+
+        def load_scale_rows(queue, dst, first, src):
+            passes = src.shape[0]
+            for q in range(4):
+                lo = 32 * q + first
+                rows = src[:, 4 * q : 4 * q + 4, :] if passes > 1 else src[0, 4 * q : 4 * q + 4, :]
+                queue.dma_start(dst[lo : lo + 4 * passes, :].bitcast(I32), rows.bitcast(I32))
+
+        def load_words(name, src):
+            words = staged(name, [P, T], U32)
+            nc.sync.dma_start(words[:].bitcast(I32), src.rearrange("p t i -> p (t i)").bitcast(I32))
+            return words
+
+        def load_rows(name, src):
+            raw = staged(name, [P, PACK, BANK], F32)
+            nc.sync.dma_start(raw[:], src.rearrange("(p j) c -> p j c", j=PACK))
+            return raw
+
+        def load_gate(dst, name, src, t0, t1):
+            rows = src.rearrange("(p t) j -> p t j", t=PACK)
+            tile = kept("%s_%d" % (name, t0), [P, t1 - t0, S], F32)
+            for q in range(4):
+                nc.sync.dma_start(tile[32 * q : 32 * q + 32, :, :], rows[:, t0:t1, :])
+            for t in range(t0, t1):
+                dst[t] = tile[:, t - t0, :]
+
+        def quantize_weight(name, raw, codes, scales):
+            dealt = cast.tile([P, BANK * PACK], BF16, name=name, tag="dealt", align_bytes=64)
+            nc.scalar.copy(
+                dealt[:].rearrange("p (t m j) -> p m j t", t=PACK, j=PACK),
+                raw[:].rearrange("p j (m t) -> p m j t", t=PACK),
+            )
+            nc.vector.quantize_mx(out=codes.bitcast(FP8X4), scales=scales, in_=dealt[:])
+
+        tab_s = kept("tab_s", [P, T], U8)
+        tab2_s = kept("tab2_s", [P, T], U8)
+        w23_s_raw = kept("w23_s_raw", [P, H], U8)
+        nc.vector.memset(w23_s_raw[:].bitcast(I32), 0)
+        nc.vector.memset(tab_s[:].bitcast(I32), 0)
+        nc.vector.memset(tab2_s[:].bitcast(I32), 0)
+
+        load_scale_rows(nc.gpsimd, w23_s_raw, 4, w3_scales)
+        load_scale_rows(nc.gpsimd, tab2_s, 0, tab2_scales)
+        idx = load_list("idx", offs)
+        idx2 = load_list("idx2", offs2)
+        idx3 = load_list("idx3", offs3)
+        idx4 = load_list("idx4", offs4)
+        gains = kept("gains", [P, 2, PACK], F32)
+        nc.sync.dma_start(gains[:], gain.rearrange("(g p t) -> p g t", g=2, t=PACK))
+        w2_raw = kept("w2_raw", [P, 2 * H], U8)
+        nc.sync.dma_start(w2_raw[:].bitcast(I32), w2_words[0].bitcast(I32))
+        tab_w = staged("tab_w", [P, T], U32)
+        for h in range(2):
+            half = slice(h * T // 2, (h + 1) * T // 2)
+            nc.sync.dma_start(
+                tab_w[:].bitcast(I32)[:, half], tab_words[0].rearrange("p t i -> p (t i)").bitcast(I32)[:, half]
+            )
+        load_scale_rows(nc.sync, tab_s, 0, tab_scales)
+        w1_raw0 = load_rows("w1_raw0", w1[:, 0:BANK])
+        load_scale_rows(nc.sync, w23_s_raw, 0, w2_scales)
+        tab2_w = [load_words("tab2_w%d" % a, tab2_words[a]) for a in range(2)]
+        w3_raw = staged("w3_raw", [P, 2, H], U32)
+        nc.sync.dma_start(
+            w3_raw[:].bitcast(I32), w3_words.rearrange("a p c i -> p a (c i)").bitcast(I32)
+        )
+        gate1 = {}
+        gate2 = {}
+        load_gate(gate1, "gate1", wg1, 0, 1)
+        w1_raw1 = load_rows("w1_raw1", w1[:, BANK : 2 * BANK])
+        load_gate(gate1, "gate1", wg1, 1, 2)
+
+        v_s = kept("v_s", [P, S], U8)
+        v_w = kept("v_w", [P, S], U32)
+        nc.vector.tensor_copy(v_w[:], tab_w[:].indirect(idx[:]))
+        nc.vector.tensor_copy(v_s[:], tab_s[:].indirect(idx[:]))
+
+        w2_c = kept("w2_c", [P, 2 * H], U8)
+        w23_s = kept("w23_s", [P, H], U8)
+        nc.vector.tensor_copy(
+            w2_c[:].rearrange("p (g t m b) -> p g t m b", g=2, t=PACK, b=2),
+            w2_raw[:].rearrange("p (g m t b) -> p g t m b", g=2, t=PACK, b=2),
+        )
+        nc.vector.tensor_copy(
+            w23_s[:].rearrange("p (g t m) -> p g t m", g=2, t=PACK),
+            w23_s_raw[:].rearrange("p (g m t) -> p g t m", g=2, t=PACK),
+        )
+        w1_c = kept("w1_c", [P, H], U32)
+        w1_s = kept("w1_s", [P, H], U8)
+        quantize_weight("w1_dealt0", w1_raw0, w1_c[:, 0:BANK], w1_s[:, 0:BANK])
+
+        w4_raw = [load_rows("w4_raw%d" % g, w4[BANK * g : BANK * (g + 1), :]) for g in range(2)]
+        load_gate(gate2, "gate2", wg2, 0, 1)
+        load_gate(gate2, "gate2", wg2, 1, 2)
+        load_gate(gate1, "gate1", wg1, 2, 4)
+        load_gate(gate2, "gate2", wg2, 2, 4)
+        v2_s = kept("v2_s", [P, S], U8)
+        v2_w = [kept("v2_w%d" % a, [P, S], U32) for a in range(2)]
+        w3_c = kept("w3_c", [P, 2, H], U32)
+        w4_c = kept("w4_c", [P, 2, N], U32)
+        w4_s = kept("w4_s", [P, 2, N], U8)
+        z_c = kept("z_c", [P, 2, T2], U32)
+        z_s = kept("z_s", [P, 2, T2], U8)
+        y_c = kept("y_c", [P, T2], U32)
+        y_s = kept("y_s", [P, T2], U8)
+
+        squares = kept("squares", [P, S], F32)
+        factor = [kept("factor%d" % k, [P, S], F32) for k in range(2)]
+        lesser = {}
+        second = {}
+        squashed = {}
+        response = {}
+        b_banks = {}
+        page = {}
+        z_bf = {}
+
+        def static_products(i):
+            rows = slice(P * i, P * (i + 1))
+            lesser[i] = work.tile([P, S], F32, name="lesser%d" % i, tag="lesser")
+            second[i] = []
+            for h in range(2):
+                cols = slice(BANK * h, BANK * (h + 1))
+                a1 = new_bank("a1_%d_%d" % (i, h))
+                nc.tensor.matmul_mx(
+                    out=a1[:], lhsT=w1_c[:, rows].bitcast(FP8X4), lhsT_scale=w1_s[:, rows],
+                    rhs=v_w[:, cols].bitcast(FP8X4), rhs_scale=v_s[:, cols], start=True, stop=True,
+                )
+                a2 = new_bank("a2_%d_%d" % (i, h))
+                nc.tensor.matmul_mx(
+                    out=a2[:], lhsT=w2_c[:, 2 * P * i : 2 * P * (i + 1)].bitcast(FP4X4), lhsT_scale=w23_s[:, rows],
+                    rhs=v_w[:, cols].bitcast(FP8X4), rhs_scale=v_s[:, cols], start=True, stop=True,
+                )
+                nc.scalar.copy(lesser[i][:, cols], a1[:])
+                second[i].append(a2)
+
+        def static_lesser(i):
+            for h in range(2):
+                cols = slice(BANK * h, BANK * (h + 1))
+                nc.vector.tensor_tensor(lesser[i][:, cols], second[i][h][:], lesser[i][:, cols], ALU.min)
+            nc.gpsimd.tensor_tensor(factor[i % 2][:], lesser[i][:], gate1[i % PACK], ALU.mult)
+
+        def static_scatter(i):
+            page[i] = pages.tile([P, T2], F32, name="page%d" % i, tag="page")
+            nc.vector.tensor_copy(page[i][:].indirect(idx3[:]), factor[i % 2][:])
+
+        def moving_products(i):
+            rows = slice(P * i, P * (i + 1))
+            squashed[i] = factor[i % 2]
+            if HYBRID:
+                response[i] = work.tile([P, S], F32, name="response%d" % i, tag="response")
+            b_banks[i] = []
+            for h in range(2):
+                cols = slice(BANK * h, BANK * (h + 1))
+                b = new_bank("b_%d_%d" % (i, h))
+                for a in range(2):
+                    nc.tensor.matmul_mx(
+                        out=b[:], lhsT=w3_c[:, a, rows].bitcast(FP8X4), lhsT_scale=w23_s[4 + 4 * a :, rows],
+                        rhs=v2_w[a][:, cols].bitcast(FP8X4), rhs_scale=v2_s[4 * a :, cols],
+                        start=(a == 0), stop=(a == 1),
+                    )
+                nc.scalar.activation(squares[:, cols], b[:], ACT.Square)
+                if HYBRID:
+                    nc.scalar.copy(response[i][:, cols], b[:])
+                b_banks[i].append(b)
+            nc.scalar.activation(squashed[i][:], squares[:], ACT.Abs_reciprocal_sqrt, bias=1.0)
+
+        def moving_factors(i):
+            if HYBRID:
+                nc.gpsimd.tensor_tensor(squashed[i][:], squashed[i][:], gate2[i % PACK], ALU.mult)
+                nc.gpsimd.tensor_tensor(response[i][:], response[i][:], squashed[i][:], ALU.mult)
+            else:
+                for h in range(2):
+                    cols = slice(BANK * h, BANK * (h + 1))
+                    nc.vector.tensor_tensor(squashed[i][:, cols], b_banks[i][h][:], squashed[i][:, cols], ALU.mult)
+
+        def moving_scatter(i):
+            if HYBRID:
+                nc.vector.tensor_copy(page[i][:].indirect(idx4[:]), response[i][:])
+            else:
+                nc.vector.tensor_tensor(page[i][:].indirect(idx4[:]), squashed[i][:], gate2[i % PACK], ALU.mult)
+
+        def round_page(i, c):
+            g, t = divmod(i, PACK)
+            if c == 0:
+                nc.scalar.copy(squares[:, 0:1], gains[:, g, t : t + 1])
+            if t == 0:
+                z_bf[g, c] = woven.tile([P, BANK, PACK], BF16, name="z_bf%d_%d" % (g, c), tag="z_bf", align_bytes=64)
+            nc.scalar.activation(
+                z_bf[g, c][:, :, t], page[i][:, BANK * c : BANK * (c + 1)], ACT.Copy, scale=squares[:, 0:1]
+            )
+
+        def quantize_z(g, c):
+            cols = slice(BANK * c, BANK * (c + 1))
+            nc.vector.quantize_mx(
+                out=z_c[:, g, cols].bitcast(FP8X4), scales=z_s[:, g, cols],
+                in_=z_bf[g, c][:].rearrange("p m t -> p (m t)"),
+            )
+
+        y_banks = {}
+
+        def project(g, c):
+            cols = slice(BANK * c, BANK * (c + 1))
+            for t in range(PACK):
+                rows = slice(P * t, P * (t + 1))
+                if g == 0:
+                    y_banks[c, t] = new_bank("y_%d_%d" % (c, t))
+                nc.tensor.matmul_mx(
+                    out=y_banks[c, t][:], lhsT=w4_c[:, g, rows].bitcast(FP8X4), lhsT_scale=w4_s[:, g, rows],
+                    rhs=z_c[:, g, cols].bitcast(FP8X4), rhs_scale=z_s[:, g, cols], start=(g == 0), stop=(g == 1),
+                )
+
+        static_products(0)
+        nc.vector.tensor_copy(v2_s[:], tab2_s[:].indirect(idx2[:]))
+        static_lesser(0)
+        static_products(1)
+        for a in range(2):
+            nc.vector.tensor_copy(v2_w[a][:], tab2_w[a][:].indirect(idx2[:]))
+        nc.vector.tensor_copy(
+            w3_c[:].bitcast(I32).rearrange("p a c -> p (a c)").rearrange("p (g t m) -> p g m t", g=4, t=PACK),
+            w3_raw[:].bitcast(I32).rearrange("p a c -> p (a c)").rearrange("p (g m t) -> p g m t", g=4, t=PACK),
+        )
+        static_scatter(0)
+        static_lesser(1)
+        static_products(2)
+        moving_products(0)
+        moving_factors(0)
+        quantize_weight("w1_dealt1", w1_raw1, w1_c[:, BANK:], w1_s[:, BANK:])
+        for g in range(2):
+            quantize_weight("w4_dealt%d" % g, w4_raw[g], w4_c[:, g, :], w4_s[:, g, :])
+        y = {}
+        for i in range(1, ROW_TILES):
+            static_scatter(i)
+            if i + 1 < ROW_TILES:
+                static_lesser(i + 1)
+            if i == 5:
+                for c in range(CHUNKS):
+                    quantize_z(0, c)
+            moving_scatter(i - 1)
+            if i + 2 < ROW_TILES:
+                static_products(i + 2)
+            moving_products(i)
+            moving_factors(i)
+            for c in range(CHUNKS):
+                round_page(i - 1, c)
+            if i == 4:
+                for c in range(CHUNKS):
+                    y[c] = load_rows("y%d" % c, up[:, BANK * c : BANK * (c + 1)])
+        last = ROW_TILES - 1
+        project(0, 0)
+        project(0, 1)
+        moving_scatter(last)
+        for c in range(CHUNKS):
+            round_page(last, c)
+
+        out_rows = out_0.rearrange("(p t) c -> p t c", t=PACK)
+        out_words = out_1[0].rearrange("p m t -> p (m t)").bitcast(I32)
+
+        def add_up(c):
+            for t in range(PACK):
+                nc.vector.tensor_tensor(y[c][:, t, :], y_banks[c, t][:], y[c][:, t, :], ALU.add)
+            nc.sync.dma_start(out_rows[:, :, BANK * c : BANK * (c + 1)], y[c][:])
+
+        y_bf = {}
+
+        def round_y(c):
+            y_bf[c] = cast.tile([P, BANK * PACK], BF16, name="y_bf%d" % c, tag="dealt", align_bytes=64)
+            nc.scalar.copy(
+                y_bf[c][:].rearrange("p (m i t) -> p m t i", i=4, t=PACK),
+                y[c][:].rearrange("p t (m i) -> p m t i", i=4),
+            )
+
+        def quantize_y(c):
+            cols = slice(BANK * c, BANK * (c + 1))
+            nc.vector.quantize_mx(out=y_c[:, cols].bitcast(FP8X4), scales=y_s[:, cols], in_=y_bf[c][:])
+            nc.sync.dma_start(out_words[:, cols], y_c[:, cols].bitcast(I32))
+
+        quantize_z(1, 0)
+        project(1, 0)
+        quantize_z(1, 1)
+        project(1, 1)
+        for c in range(CHUNKS):
+            add_up(c)
+            round_y(c)
+            if c + 2 < CHUNKS:
+                quantize_z(1, c + 2)
+                project(0, c + 2)
+                project(1, c + 2)
+            if c >= 1:
+                quantize_y(c - 1)
+        quantize_y(CHUNKS - 1)
+        for q in range(4):
+            nc.sync.dma_start(
+                out_2[0, 4 * q : 4 * q + 4, :].bitcast(I32), y_s[32 * q : 32 * q + 4, :].bitcast(I32)
+            )

@@ -21,7 +21,6 @@ PACK = 4
 BANK = 512
 ROW_TILES = H // P
 CHUNKS = T2 // BANK
-HYBRID = True
 
 
 def tile_list_woven_video_residual_kernel(
@@ -35,17 +34,13 @@ def tile_list_woven_video_residual_kernel(
         cast = ctx.enter_context(tc.tile_pool(name="cast", bufs=2))
         pages = ctx.enter_context(tc.tile_pool(name="pages", bufs=3))
         woven = ctx.enter_context(tc.tile_pool(name="woven", bufs=CHUNKS))
-        work = ctx.enter_context(tc.tile_pool(name="work", bufs=2))
-        psum = ctx.enter_context(tc.psum_pool(name="psum", bufs=8))
+        psum = ctx.enter_context(tc.psum_pool(name="psum", bufs=1))
 
         def kept(name, shape, dtype):
             return keep.tile(shape, dtype, name=name, align_bytes=64)
 
         def staged(name, shape, dtype):
             return big.tile(shape, dtype, name=name, tag="big", align_bytes=64)
-
-        def new_bank(name):
-            return psum.tile([P, BANK], F32, name=name, tag="bank")
 
         def load_list(name, src):
             lst = keep.tile([P, S // 16], U16, name=name)
@@ -88,44 +83,38 @@ def tile_list_woven_video_residual_kernel(
         tab_s = kept("tab_s", [P, T], U8)
         tab2_s = kept("tab2_s", [P, T], U8)
         w23_s_raw = kept("w23_s_raw", [P, H], U8)
-        nc.vector.memset(w23_s_raw[:].bitcast(I32), 0)
         nc.vector.memset(tab_s[:].bitcast(I32), 0)
+        nc.vector.memset(w23_s_raw[:].bitcast(I32), 0)
         nc.vector.memset(tab2_s[:].bitcast(I32), 0)
 
-        load_scale_rows(nc.gpsimd, w23_s_raw, 4, w3_scales)
-        load_scale_rows(nc.gpsimd, tab2_s, 0, tab2_scales)
         idx = load_list("idx", offs)
         idx2 = load_list("idx2", offs2)
-        idx3 = load_list("idx3", offs3)
-        idx4 = load_list("idx4", offs4)
-        gains = kept("gains", [P, 2, PACK], F32)
-        nc.sync.dma_start(gains[:], gain.rearrange("(g p t) -> p g t", g=2, t=PACK))
         w2_raw = kept("w2_raw", [P, 2 * H], U8)
         nc.sync.dma_start(w2_raw[:].bitcast(I32), w2_words[0].bitcast(I32))
-        tab_w = staged("tab_w", [P, T], U32)
-        for h in range(2):
-            half = slice(h * T // 2, (h + 1) * T // 2)
-            nc.sync.dma_start(
-                tab_w[:].bitcast(I32)[:, half], tab_words[0].rearrange("p t i -> p (t i)").bitcast(I32)[:, half]
-            )
         load_scale_rows(nc.sync, tab_s, 0, tab_scales)
+        tab_w = load_words("tab_w", tab_words[0])
         w1_raw0 = load_rows("w1_raw0", w1[:, 0:BANK])
         load_scale_rows(nc.sync, w23_s_raw, 0, w2_scales)
-        tab2_w = [load_words("tab2_w%d" % a, tab2_words[a]) for a in range(2)]
+        tab2_w = [load_words("tab2_w0", tab2_words[0])]
+        load_scale_rows(nc.sync, w23_s_raw, 4, w3_scales)
+        tab2_w.append(load_words("tab2_w1", tab2_words[1]))
+        load_scale_rows(nc.sync, tab2_s, 0, tab2_scales)
         w3_raw = staged("w3_raw", [P, 2, H], U32)
         nc.sync.dma_start(
             w3_raw[:].bitcast(I32), w3_words.rearrange("a p c i -> p a (c i)").bitcast(I32)
         )
+        idx3 = load_list("idx3", offs3)
         gate1 = {}
         gate2 = {}
         load_gate(gate1, "gate1", wg1, 0, 1)
-        w1_raw1 = load_rows("w1_raw1", w1[:, BANK : 2 * BANK])
         load_gate(gate1, "gate1", wg1, 1, 2)
+        w1_raw1 = load_rows("w1_raw1", w1[:, BANK : 2 * BANK])
+        idx4 = load_list("idx4", offs4)
 
         v_s = kept("v_s", [P, S], U8)
         v_w = kept("v_w", [P, S], U32)
-        nc.vector.tensor_copy(v_w[:], tab_w[:].indirect(idx[:]))
         nc.vector.tensor_copy(v_s[:], tab_s[:].indirect(idx[:]))
+        nc.vector.tensor_copy(v_w[:], tab_w[:].indirect(idx[:]))
 
         w2_c = kept("w2_c", [P, 2 * H], U8)
         w23_s = kept("w23_s", [P, H], U8)
@@ -143,6 +132,8 @@ def tile_list_woven_video_residual_kernel(
 
         w4_raw = [load_rows("w4_raw%d" % g, w4[BANK * g : BANK * (g + 1), :]) for g in range(2)]
         load_gate(gate2, "gate2", wg2, 0, 1)
+        gains = kept("gains", [P, 2, PACK], F32)
+        nc.sync.dma_start(gains[:], gain.rearrange("(g p t) -> p g t", g=2, t=PACK))
         load_gate(gate2, "gate2", wg2, 1, 2)
         load_gate(gate1, "gate1", wg1, 2, 4)
         load_gate(gate2, "gate2", wg2, 2, 4)
@@ -157,89 +148,72 @@ def tile_list_woven_video_residual_kernel(
         y_s = kept("y_s", [P, T2], U8)
 
         squares = kept("squares", [P, S], F32)
+        first_sums = kept("first_sums", [P, S], F32)
         factor = [kept("factor%d" % k, [P, S], F32) for k in range(2)]
-        lesser = {}
-        second = {}
-        squashed = {}
-        response = {}
-        b_banks = {}
+        stream = [kept("stream%d" % k, [P, S], F32) for k in range(3)]
+        banks = [psum.tile([P, BANK], F32, name="bank%d" % k) for k in range(8)]
+        last = ROW_TILES - 1
         page = {}
         z_bf = {}
 
         def static_products(i):
             rows = slice(P * i, P * (i + 1))
-            lesser[i] = work.tile([P, S], F32, name="lesser%d" % i, tag="lesser")
-            second[i] = []
             for h in range(2):
                 cols = slice(BANK * h, BANK * (h + 1))
-                a1 = new_bank("a1_%d_%d" % (i, h))
                 nc.tensor.matmul_mx(
-                    out=a1[:], lhsT=w1_c[:, rows].bitcast(FP8X4), lhsT_scale=w1_s[:, rows],
+                    out=banks[h][:], lhsT=w1_c[:, rows].bitcast(FP8X4), lhsT_scale=w1_s[:, rows],
                     rhs=v_w[:, cols].bitcast(FP8X4), rhs_scale=v_s[:, cols], start=True, stop=True,
                 )
-                a2 = new_bank("a2_%d_%d" % (i, h))
                 nc.tensor.matmul_mx(
-                    out=a2[:], lhsT=w2_c[:, 2 * P * i : 2 * P * (i + 1)].bitcast(FP4X4), lhsT_scale=w23_s[:, rows],
+                    out=banks[2 + h][:], lhsT=w2_c[:, 2 * P * i : 2 * P * (i + 1)].bitcast(FP4X4),
+                    lhsT_scale=w23_s[:, rows],
                     rhs=v_w[:, cols].bitcast(FP8X4), rhs_scale=v_s[:, cols], start=True, stop=True,
                 )
-                nc.scalar.copy(lesser[i][:, cols], a1[:])
-                second[i].append(a2)
+                nc.scalar.copy(first_sums[:, cols], banks[h][:])
 
         def static_lesser(i):
             for h in range(2):
                 cols = slice(BANK * h, BANK * (h + 1))
-                nc.vector.tensor_tensor(lesser[i][:, cols], second[i][h][:], lesser[i][:, cols], ALU.min)
-            nc.gpsimd.tensor_tensor(factor[i % 2][:], lesser[i][:], gate1[i % PACK], ALU.mult)
+                nc.vector.tensor_tensor(stream[i % 3][:, cols], banks[2 + h][:], first_sums[:, cols], ALU.min)
+            nc.gpsimd.tensor_tensor(factor[i % 2][:], stream[i % 3][:], gate1[i % PACK], ALU.mult)
 
         def static_scatter(i):
             page[i] = pages.tile([P, T2], F32, name="page%d" % i, tag="page")
             nc.vector.tensor_copy(page[i][:].indirect(idx3[:]), factor[i % 2][:])
 
-        def moving_products(i):
+        def moving_values(i):
             rows = slice(P * i, P * (i + 1))
-            squashed[i] = factor[i % 2]
-            if HYBRID:
-                response[i] = work.tile([P, S], F32, name="response%d" % i, tag="response")
-            b_banks[i] = []
+            response = stream[i % 3]
+            squared = squares
+            damping = first_sums if i == last else factor[i % 2]
             for h in range(2):
                 cols = slice(BANK * h, BANK * (h + 1))
-                b = new_bank("b_%d_%d" % (i, h))
                 for a in range(2):
                     nc.tensor.matmul_mx(
-                        out=b[:], lhsT=w3_c[:, a, rows].bitcast(FP8X4), lhsT_scale=w23_s[4 + 4 * a :, rows],
+                        out=banks[h][:], lhsT=w3_c[:, a, rows].bitcast(FP8X4), lhsT_scale=w23_s[4 + 4 * a :, rows],
                         rhs=v2_w[a][:, cols].bitcast(FP8X4), rhs_scale=v2_s[4 * a :, cols],
                         start=(a == 0), stop=(a == 1),
                     )
-                nc.scalar.activation(squares[:, cols], b[:], ACT.Square)
-                if HYBRID:
-                    nc.scalar.copy(response[i][:, cols], b[:])
-                b_banks[i].append(b)
-            nc.scalar.activation(squashed[i][:], squares[:], ACT.Abs_reciprocal_sqrt, bias=1.0)
-
-        def moving_factors(i):
-            if HYBRID:
-                nc.gpsimd.tensor_tensor(squashed[i][:], squashed[i][:], gate2[i % PACK], ALU.mult)
-                nc.gpsimd.tensor_tensor(response[i][:], response[i][:], squashed[i][:], ALU.mult)
-            else:
-                for h in range(2):
-                    cols = slice(BANK * h, BANK * (h + 1))
-                    nc.vector.tensor_tensor(squashed[i][:, cols], b_banks[i][h][:], squashed[i][:, cols], ALU.mult)
+                nc.scalar.copy(response[:, cols], banks[h][:])
+            nc.scalar.activation(squared[:], response[:], ACT.Square)
+            nc.scalar.activation(damping[:], squared[:], ACT.Abs_reciprocal_sqrt, bias=1.0)
+            nc.gpsimd.tensor_tensor(damping[:], damping[:], gate2[i % PACK], ALU.mult)
+            nc.gpsimd.tensor_tensor(response[:], response[:], damping[:], ALU.mult)
 
         def moving_scatter(i):
-            if HYBRID:
-                nc.vector.tensor_copy(page[i][:].indirect(idx4[:]), response[i][:])
-            else:
-                nc.vector.tensor_tensor(page[i][:].indirect(idx4[:]), squashed[i][:], gate2[i % PACK], ALU.mult)
+            nc.vector.tensor_copy(page[i][:].indirect(idx4[:]), stream[i % 3][:])
 
-        def round_page(i, c):
+        def round_page(i):
             g, t = divmod(i, PACK)
-            if c == 0:
-                nc.scalar.copy(squares[:, 0:1], gains[:, g, t : t + 1])
-            if t == 0:
-                z_bf[g, c] = woven.tile([P, BANK, PACK], BF16, name="z_bf%d_%d" % (g, c), tag="z_bf", align_bytes=64)
-            nc.scalar.activation(
-                z_bf[g, c][:, :, t], page[i][:, BANK * c : BANK * (c + 1)], ACT.Copy, scale=squares[:, 0:1]
-            )
+            nc.scalar.copy(squares[:, 0:1], gains[:, g, t : t + 1])
+            for c in range(CHUNKS):
+                if t == 0:
+                    z_bf[g, c] = woven.tile([P, BANK, PACK], BF16, name="z_bf%d_%d" % (g, c), tag="z_bf", align_bytes=64)
+                rows = page[i][:, BANK * c : BANK * (c + 1)]
+                if i == last and c < 2:
+                    nc.vector.tensor_scalar(z_bf[g, c][:, :, t], rows, squares[:, 0:1], None, ALU.mult)
+                else:
+                    nc.scalar.activation(z_bf[g, c][:, :, t], rows, ACT.Copy, scale=squares[:, 0:1])
 
         def quantize_z(g, c):
             cols = slice(BANK * c, BANK * (c + 1))
@@ -248,98 +222,95 @@ def tile_list_woven_video_residual_kernel(
                 in_=z_bf[g, c][:].rearrange("p m t -> p (m t)"),
             )
 
-        y_banks = {}
+        def y_bank(c, t):
+            return banks[PACK * ((c + 1) % 2) + t]
 
         def project(g, c):
             cols = slice(BANK * c, BANK * (c + 1))
             for t in range(PACK):
                 rows = slice(P * t, P * (t + 1))
-                if g == 0:
-                    y_banks[c, t] = new_bank("y_%d_%d" % (c, t))
                 nc.tensor.matmul_mx(
-                    out=y_banks[c, t][:], lhsT=w4_c[:, g, rows].bitcast(FP8X4), lhsT_scale=w4_s[:, g, rows],
+                    out=y_bank(c, t)[:], lhsT=w4_c[:, g, rows].bitcast(FP8X4), lhsT_scale=w4_s[:, g, rows],
                     rhs=z_c[:, g, cols].bitcast(FP8X4), rhs_scale=z_s[:, g, cols], start=(g == 0), stop=(g == 1),
                 )
 
         static_products(0)
-        nc.vector.tensor_copy(v2_s[:], tab2_s[:].indirect(idx2[:]))
+        nc.vector.tensor_copy(v2_w[0][:], tab2_w[0][:].indirect(idx2[:]))
         static_lesser(0)
         static_products(1)
-        for a in range(2):
-            nc.vector.tensor_copy(v2_w[a][:], tab2_w[a][:].indirect(idx2[:]))
+        nc.vector.tensor_copy(v2_w[1][:], tab2_w[1][:].indirect(idx2[:]))
+        nc.vector.tensor_copy(v2_s[:], tab2_s[:].indirect(idx2[:]))
         nc.vector.tensor_copy(
             w3_c[:].bitcast(I32).rearrange("p a c -> p (a c)").rearrange("p (g t m) -> p g m t", g=4, t=PACK),
             w3_raw[:].bitcast(I32).rearrange("p a c -> p (a c)").rearrange("p (g m t) -> p g m t", g=4, t=PACK),
         )
-        static_scatter(0)
         static_lesser(1)
+        static_scatter(0)
+        moving_values(0)
         static_products(2)
-        moving_products(0)
-        moving_factors(0)
         quantize_weight("w1_dealt1", w1_raw1, w1_c[:, BANK:], w1_s[:, BANK:])
         for g in range(2):
             quantize_weight("w4_dealt%d" % g, w4_raw[g], w4_c[:, g, :], w4_s[:, g, :])
-        y = {}
+        y = [load_rows("y%d" % c, up[:, BANK * c : BANK * (c + 1)]) for c in range(CHUNKS)]
         for i in range(1, ROW_TILES):
             static_scatter(i)
             if i + 1 < ROW_TILES:
                 static_lesser(i + 1)
-            if i == 5:
+            if i == PACK + 1:
                 for c in range(CHUNKS):
                     quantize_z(0, c)
+                project(0, 0)
             moving_scatter(i - 1)
+            if i < last:
+                moving_values(i)
             if i + 2 < ROW_TILES:
                 static_products(i + 2)
-            moving_products(i)
-            moving_factors(i)
-            for c in range(CHUNKS):
-                round_page(i - 1, c)
-            if i == 4:
-                for c in range(CHUNKS):
-                    y[c] = load_rows("y%d" % c, up[:, BANK * c : BANK * (c + 1)])
-        last = ROW_TILES - 1
-        project(0, 0)
+            if i + 1 == last:
+                moving_values(last)
+            round_page(i - 1)
         project(0, 1)
         moving_scatter(last)
-        for c in range(CHUNKS):
-            round_page(last, c)
+        round_page(last)
 
         out_rows = out_0.rearrange("(p t) c -> p t c", t=PACK)
         out_words = out_1[0].rearrange("p m t -> p (m t)").bitcast(I32)
 
-        def add_up(c):
-            for t in range(PACK):
-                nc.vector.tensor_tensor(y[c][:, t, :], y_banks[c, t][:], y[c][:, t, :], ALU.add)
-            nc.sync.dma_start(out_rows[:, :, BANK * c : BANK * (c + 1)], y[c][:])
-
+        pieces = [(0, 0, 512), (1, 0, 512), (2, 0, 512), (3, 0, 256), (3, 256, 512)]
         y_bf = {}
 
-        def round_y(c):
-            y_bf[c] = cast.tile([P, BANK * PACK], BF16, name="y_bf%d" % c, tag="dealt", align_bytes=64)
+        def add_up(c, lo, hi):
+            cols = slice(BANK * c + lo, BANK * c + hi)
+            for t in range(PACK):
+                nc.vector.tensor_tensor(y[c][:, t, lo:hi], y_bank(c, t)[:, lo:hi], y[c][:, t, lo:hi], ALU.add)
+                if t % 2 == 1:
+                    nc.sync.dma_start(out_rows[:, t - 1 : t + 1, cols], y[c][:, t - 1 : t + 1, lo:hi])
+            y_bf[c, lo] = woven.tile([P, hi - lo, PACK], BF16, name="y_bf%d_%d" % (c, lo), tag="z_bf", align_bytes=64)
             nc.scalar.copy(
-                y_bf[c][:].rearrange("p (m i t) -> p m t i", i=4, t=PACK),
-                y[c][:].rearrange("p t (m i) -> p m t i", i=4),
+                y_bf[c, lo][:].rearrange("p (m i) t -> p m t i", i=4),
+                y[c][:, :, lo:hi].rearrange("p t (m i) -> p m t i", i=4),
             )
 
-        def quantize_y(c):
-            cols = slice(BANK * c, BANK * (c + 1))
-            nc.vector.quantize_mx(out=y_c[:, cols].bitcast(FP8X4), scales=y_s[:, cols], in_=y_bf[c][:])
+        def quantize_y(c, lo, hi):
+            cols = slice(BANK * c + lo, BANK * c + hi)
+            nc.vector.quantize_mx(
+                out=y_c[:, cols].bitcast(FP8X4), scales=y_s[:, cols], in_=y_bf[c, lo][:].rearrange("p m t -> p (m t)")
+            )
             nc.sync.dma_start(out_words[:, cols], y_c[:, cols].bitcast(I32))
 
         quantize_z(1, 0)
         project(1, 0)
         quantize_z(1, 1)
         project(1, 1)
-        for c in range(CHUNKS):
-            add_up(c)
-            round_y(c)
-            if c + 2 < CHUNKS:
+        for n, (c, lo, hi) in enumerate(pieces):
+            add_up(c, lo, hi)
+            if c + 2 < CHUNKS and hi == BANK:
                 quantize_z(1, c + 2)
                 project(0, c + 2)
                 project(1, c + 2)
-            if c >= 1:
-                quantize_y(c - 1)
-        quantize_y(CHUNKS - 1)
+            if n >= 2:
+                quantize_y(*pieces[n - 2])
+        for piece in pieces[len(pieces) - 2 :]:
+            quantize_y(*piece)
         for q in range(4):
             nc.sync.dma_start(
                 out_2[0, 4 * q : 4 * q + 4, :].bitcast(I32), y_s[32 * q : 32 * q + 4, :].bitcast(I32)

@@ -108,8 +108,9 @@ def tile_list_woven_video_residual_kernel(
         gate2 = {}
         load_gate(gate1, "gate1", wg1, 0, 1)
         load_gate(gate1, "gate1", wg1, 1, 2)
-        w1_raw1 = load_rows("w1_raw1", w1[:, BANK : 2 * BANK])
         idx4 = load_list("idx4", offs4)
+        load_gate(gate2, "gate2", wg2, 0, 1)
+        w1_raw1 = load_rows("w1_raw1", w1[:, BANK : 2 * BANK])
 
         v_s = kept("v_s", [P, S], U8)
         v_w = kept("v_w", [P, S], U32)
@@ -130,13 +131,13 @@ def tile_list_woven_video_residual_kernel(
         w1_s = kept("w1_s", [P, H], U8)
         quantize_weight("w1_dealt0", w1_raw0, w1_c[:, 0:BANK], w1_s[:, 0:BANK])
 
-        w4_raw = [load_rows("w4_raw%d" % g, w4[BANK * g : BANK * (g + 1), :]) for g in range(2)]
-        load_gate(gate2, "gate2", wg2, 0, 1)
         gains = kept("gains", [P, 2, PACK], F32)
         nc.sync.dma_start(gains[:], gain.rearrange("(g p t) -> p g t", g=2, t=PACK))
         load_gate(gate2, "gate2", wg2, 1, 2)
         load_gate(gate1, "gate1", wg1, 2, 4)
         load_gate(gate2, "gate2", wg2, 2, 4)
+        w4_raw = [load_rows("w4_raw0", w4[0:BANK, :])]
+        w4_raw.append(load_rows("w4_raw1", w4[BANK : 2 * BANK, :]))
         v2_s = kept("v2_s", [P, S], U8)
         v2_w = [kept("v2_w%d" % a, [P, S], U32) for a in range(2)]
         w3_c = kept("w3_c", [P, 2, H], U32)
@@ -153,6 +154,7 @@ def tile_list_woven_video_residual_kernel(
         stream = [kept("stream%d" % k, [P, S], F32) for k in range(3)]
         banks = [psum.tile([P, BANK], F32, name="bank%d" % k) for k in range(8)]
         last = ROW_TILES - 1
+        halves = [slice(0, BANK), slice(BANK, S)]
         page = {}
         z_bf = {}
 
@@ -195,25 +197,29 @@ def tile_list_woven_video_residual_kernel(
                         start=(a == 0), stop=(a == 1),
                     )
                 nc.scalar.copy(response[:, cols], banks[h][:])
-            nc.scalar.activation(squared[:], response[:], ACT.Square)
-            nc.scalar.activation(damping[:], squared[:], ACT.Abs_reciprocal_sqrt, bias=1.0)
-            nc.gpsimd.tensor_tensor(damping[:], damping[:], gate2[i % PACK], ALU.mult)
-            nc.gpsimd.tensor_tensor(response[:], response[:], damping[:], ALU.mult)
+            for cols in halves:
+                nc.scalar.activation(squared[:, cols], response[:, cols], ACT.Square)
+            for cols in halves:
+                nc.scalar.activation(damping[:, cols], squared[:, cols], ACT.Abs_reciprocal_sqrt, bias=1.0)
+            for cols in halves:
+                nc.gpsimd.tensor_tensor(damping[:, cols], damping[:, cols], gate2[i % PACK][:, cols], ALU.mult)
+            for cols in halves:
+                nc.gpsimd.tensor_tensor(response[:, cols], response[:, cols], damping[:, cols], ALU.mult)
 
         def moving_scatter(i):
             nc.vector.tensor_copy(page[i][:].indirect(idx4[:]), stream[i % 3][:])
 
         def round_page(i):
             g, t = divmod(i, PACK)
-            nc.scalar.copy(squares[:, 0:1], gains[:, g, t : t + 1])
+            nc.scalar.copy(squares[:, S - 1 : S], gains[:, g, t : t + 1])
             for c in range(CHUNKS):
                 if t == 0:
                     z_bf[g, c] = woven.tile([P, BANK, PACK], BF16, name="z_bf%d_%d" % (g, c), tag="z_bf", align_bytes=64)
                 rows = page[i][:, BANK * c : BANK * (c + 1)]
-                if i == last and c < 2:
-                    nc.vector.tensor_scalar(z_bf[g, c][:, :, t], rows, squares[:, 0:1], None, ALU.mult)
+                if i == last and c < 1:
+                    nc.vector.tensor_scalar(z_bf[g, c][:, :, t], rows, squares[:, S - 1 : S], None, ALU.mult)
                 else:
-                    nc.scalar.activation(z_bf[g, c][:, :, t], rows, ACT.Copy, scale=squares[:, 0:1])
+                    nc.scalar.activation(z_bf[g, c][:, :, t], rows, ACT.Copy, scale=squares[:, S - 1 : S])
 
         def quantize_z(g, c):
             cols = slice(BANK * c, BANK * (c + 1))
@@ -249,8 +255,6 @@ def tile_list_woven_video_residual_kernel(
         moving_values(0)
         static_products(2)
         quantize_weight("w1_dealt1", w1_raw1, w1_c[:, BANK:], w1_s[:, BANK:])
-        for g in range(2):
-            quantize_weight("w4_dealt%d" % g, w4_raw[g], w4_c[:, g, :], w4_s[:, g, :])
         y = [load_rows("y%d" % c, up[:, BANK * c : BANK * (c + 1)]) for c in range(CHUNKS)]
         for i in range(1, ROW_TILES):
             static_scatter(i)
@@ -265,6 +269,9 @@ def tile_list_woven_video_residual_kernel(
                 moving_values(i)
             if i + 2 < ROW_TILES:
                 static_products(i + 2)
+            if i in (3, 4):
+                g = i - 3
+                quantize_weight("w4_dealt%d" % g, w4_raw[g], w4_c[:, g, :], w4_s[:, g, :])
             if i + 1 == last:
                 moving_values(last)
             round_page(i - 1)

@@ -1,3 +1,4 @@
+import itertools
 from contextlib import ExitStack
 
 import concourse.mybir as mybir
@@ -19,8 +20,16 @@ ACT = mybir.ActivationFunctionType
 P = 128
 PACK = 4
 BANK = 512
+QUADRANTS = 4
+LINE = 4
 ROW_TILES = H // P
+LAST = ROW_TILES - 1
 CHUNKS = T2 // BANK
+STAGE_SLOTS = 6
+PAGES = 3
+STREAM_TILES = 3
+W4_STEP = 3
+Y_LAG = 2
 
 
 def tile_list_woven_video_residual_kernel(
@@ -28,33 +37,38 @@ def tile_list_woven_video_residual_kernel(
     w2_words, w2_scales, w3_words, w3_scales, wg1, wg2, gain, w4, up, out_0, out_1, out_2,
 ):
     nc = tc.nc
+    halves = (slice(0, BANK), slice(BANK, S))
+    pieces = [(c, 0, BANK) for c in range(CHUNKS - 1)] + [(CHUNKS - 1, 0, BANK // 2), (CHUNKS - 1, BANK // 2, BANK)]
     with ExitStack() as ctx:
         keep = ctx.enter_context(tc.tile_pool(name="keep", bufs=1))
-        big = ctx.enter_context(tc.tile_pool(name="big", bufs=6))
-        cast = ctx.enter_context(tc.tile_pool(name="cast", bufs=2))
-        pages = ctx.enter_context(tc.tile_pool(name="pages", bufs=3))
-        woven = ctx.enter_context(tc.tile_pool(name="woven", bufs=CHUNKS))
+        stage = ctx.enter_context(tc.tile_pool(name="stage", bufs=STAGE_SLOTS))
+        dealt_pool = ctx.enter_context(tc.tile_pool(name="dealt", bufs=2))
+        page_pool = ctx.enter_context(tc.tile_pool(name="pages", bufs=PAGES))
+        woven_pool = ctx.enter_context(tc.tile_pool(name="woven", bufs=CHUNKS))
         psum = ctx.enter_context(tc.psum_pool(name="psum", bufs=1))
 
         def kept(name, shape, dtype):
             return keep.tile(shape, dtype, name=name, align_bytes=64)
 
         def staged(name, shape, dtype):
-            return big.tile(shape, dtype, name=name, tag="big", align_bytes=64)
+            return stage.tile(shape, dtype, name=name, tag="stage", align_bytes=64)
+
+        def woven(name, columns):
+            return woven_pool.tile([P, columns, PACK], BF16, name=name, tag="woven", align_bytes=64)
 
         def load_list(name, src):
-            lst = keep.tile([P, S // 16], U16, name=name)
-            nc.sync.dma_start(lst[:], src)
-            return lst
+            offsets = keep.tile([P, S // 16], U16, name=name)
+            nc.sync.dma_start(offsets[:], src)
+            return offsets
 
-        def load_scale_rows(queue, dst, first, src):
+        def load_scale_rows(dst, first, src):
             passes = src.shape[0]
-            for q in range(4):
-                lo = 32 * q + first
-                rows = src[:, 4 * q : 4 * q + 4, :] if passes > 1 else src[0, 4 * q : 4 * q + 4, :]
-                queue.dma_start(dst[lo : lo + 4 * passes, :].bitcast(I32), rows.bitcast(I32))
+            for q in range(QUADRANTS):
+                start = 32 * q + first
+                scale_rows = src[:, 4 * q : 4 * q + 4, :] if passes > 1 else src[0, 4 * q : 4 * q + 4, :]
+                nc.sync.dma_start(dst[start : start + 4 * passes, :].bitcast(I32), scale_rows.bitcast(I32))
 
-        def load_words(name, src):
+        def load_table_words(name, src):
             words = staged(name, [P, T], U32)
             nc.sync.dma_start(words[:].bitcast(I32), src.rearrange("p t i -> p (t i)").bitcast(I32))
             return words
@@ -64,19 +78,19 @@ def tile_list_woven_video_residual_kernel(
             nc.sync.dma_start(raw[:], src.rearrange("(p j) c -> p j c", j=PACK))
             return raw
 
-        def load_gate(dst, name, src, t0, t1):
-            rows = src.rearrange("(p t) j -> p t j", t=PACK)
+        def load_gate(gate, name, src, t0, t1):
+            by_slot = src.rearrange("(p t) j -> p t j", t=PACK)
             tile = kept("%s_%d" % (name, t0), [P, t1 - t0, S], F32)
-            for q in range(4):
-                nc.sync.dma_start(tile[32 * q : 32 * q + 32, :, :], rows[:, t0:t1, :])
+            for q in range(QUADRANTS):
+                nc.sync.dma_start(tile[32 * q : 32 * q + 32, :, :], by_slot[:, t0:t1, :])
             for t in range(t0, t1):
-                dst[t] = tile[:, t - t0, :]
+                gate[t] = tile[:, t - t0, :]
 
         def quantize_weight(name, raw, codes, scales):
-            dealt = cast.tile([P, BANK * PACK], BF16, name=name, tag="dealt", align_bytes=64)
+            dealt = dealt_pool.tile([P, BANK * PACK], BF16, name=name, tag="dealt", align_bytes=64)
             nc.scalar.copy(
-                dealt[:].rearrange("p (t m j) -> p m j t", t=PACK, j=PACK),
-                raw[:].rearrange("p j (m t) -> p m j t", t=PACK),
+                dealt[:].rearrange("p (t m j) -> p m t j", t=PACK, j=PACK),
+                raw[:].rearrange("p j (m t) -> p m t j", t=PACK),
             )
             nc.vector.quantize_mx(out=codes.bitcast(FP8X4), scales=scales, in_=dealt[:])
 
@@ -84,37 +98,37 @@ def tile_list_woven_video_residual_kernel(
         tab2_s = kept("tab2_s", [P, T], U8)
         w23_s_raw = kept("w23_s_raw", [P, H], U8)
         nc.vector.memset(tab_s[:].bitcast(I32), 0)
-        nc.vector.memset(w23_s_raw[:].bitcast(I32), 0)
         nc.vector.memset(tab2_s[:].bitcast(I32), 0)
+        nc.vector.memset(w23_s_raw[:].bitcast(I32), 0)
 
-        idx = load_list("idx", offs)
-        idx2 = load_list("idx2", offs2)
-        w2_raw = kept("w2_raw", [P, 2 * H], U8)
-        nc.sync.dma_start(w2_raw[:].bitcast(I32), w2_words[0].bitcast(I32))
-        load_scale_rows(nc.sync, tab_s, 0, tab_scales)
-        tab_w = load_words("tab_w", tab_words[0])
-        w1_raw0 = load_rows("w1_raw0", w1[:, 0:BANK])
-        load_scale_rows(nc.sync, w23_s_raw, 0, w2_scales)
-        tab2_w = [load_words("tab2_w0", tab2_words[0])]
-        load_scale_rows(nc.sync, w23_s_raw, 4, w3_scales)
-        tab2_w.append(load_words("tab2_w1", tab2_words[1]))
-        load_scale_rows(nc.sync, tab2_s, 0, tab2_scales)
-        w3_raw = staged("w3_raw", [P, 2, H], U32)
-        nc.sync.dma_start(
-            w3_raw[:].bitcast(I32), w3_words.rearrange("a p c i -> p a (c i)").bitcast(I32)
-        )
-        idx3 = load_list("idx3", offs3)
         gate1 = {}
         gate2 = {}
+        w2_raw = kept("w2_raw", [P, 2 * H], U8)
+        idx = load_list("idx", offs)
+        idx2 = load_list("idx2", offs2)
+        nc.sync.dma_start(w2_raw[:].bitcast(I32), w2_words[0].bitcast(I32))
+        load_scale_rows(tab_s, 0, tab_scales)
+        tab_w = load_table_words("tab_w", tab_words[0])
+        load_scale_rows(tab2_s, 0, tab2_scales)
+        w1_raw = [load_rows("w1_raw0", w1[:, 0:BANK])]
+        load_scale_rows(w23_s_raw, 0, w2_scales)
+        tab2_w = [load_table_words("tab2_w0", tab2_words[0])]
+        load_scale_rows(w23_s_raw, 4, w3_scales)
+        tab2_w.append(load_table_words("tab2_w1", tab2_words[1]))
+        w3_raw = staged("w3_raw", [P, 2, H], U32)
+        nc.sync.dma_start(w3_raw[:].bitcast(I32), w3_words.rearrange("a p c i -> p a (c i)").bitcast(I32))
+        idx3 = load_list("idx3", offs3)
         load_gate(gate1, "gate1", wg1, 0, 1)
         load_gate(gate1, "gate1", wg1, 1, 2)
         idx4 = load_list("idx4", offs4)
         load_gate(gate2, "gate2", wg2, 0, 1)
-        w1_raw1 = load_rows("w1_raw1", w1[:, BANK : 2 * BANK])
+        w1_raw.append(load_rows("w1_raw1", w1[:, BANK : 2 * BANK]))
 
         v_s = kept("v_s", [P, S], U8)
         v_w = kept("v_w", [P, S], U32)
         nc.vector.tensor_copy(v_s[:], tab_s[:].indirect(idx[:]))
+        v2_s = kept("v2_s", [P, S], U8)
+        nc.vector.tensor_copy(v2_s[:], tab2_s[:].indirect(idx2[:]))
         nc.vector.tensor_copy(v_w[:], tab_w[:].indirect(idx[:]))
 
         w2_c = kept("w2_c", [P, 2 * H], U8)
@@ -129,16 +143,15 @@ def tile_list_woven_video_residual_kernel(
         )
         w1_c = kept("w1_c", [P, H], U32)
         w1_s = kept("w1_s", [P, H], U8)
-        quantize_weight("w1_dealt0", w1_raw0, w1_c[:, 0:BANK], w1_s[:, 0:BANK])
+        quantize_weight("w1_dealt0", w1_raw[0], w1_c[:, 0:BANK], w1_s[:, 0:BANK])
 
         gains = kept("gains", [P, 2, PACK], F32)
         nc.sync.dma_start(gains[:], gain.rearrange("(g p t) -> p g t", g=2, t=PACK))
         load_gate(gate2, "gate2", wg2, 1, 2)
-        load_gate(gate1, "gate1", wg1, 2, 4)
-        load_gate(gate2, "gate2", wg2, 2, 4)
-        w4_raw = [load_rows("w4_raw0", w4[0:BANK, :])]
-        w4_raw.append(load_rows("w4_raw1", w4[BANK : 2 * BANK, :]))
-        v2_s = kept("v2_s", [P, S], U8)
+        load_gate(gate1, "gate1", wg1, 2, PACK)
+        load_gate(gate2, "gate2", wg2, 2, PACK)
+        w4_raw = [load_rows("w4_raw%d" % g, w4[BANK * g : BANK * (g + 1), :]) for g in range(2)]
+
         v2_w = [kept("v2_w%d" % a, [P, S], U32) for a in range(2)]
         w3_c = kept("w3_c", [P, 2, H], U32)
         w4_c = kept("w4_c", [P, 2, N], U32)
@@ -149,19 +162,18 @@ def tile_list_woven_video_residual_kernel(
         y_s = kept("y_s", [P, T2], U8)
 
         squares = kept("squares", [P, S], F32)
-        first_sums = kept("first_sums", [P, S], F32)
+        gain_column = squares[:, S - 1 : S]
+        w1_sums = kept("w1_sums", [P, S], F32)
         factor = [kept("factor%d" % k, [P, S], F32) for k in range(2)]
-        stream = [kept("stream%d" % k, [P, S], F32) for k in range(3)]
-        banks = [psum.tile([P, BANK], F32, name="bank%d" % k) for k in range(8)]
-        last = ROW_TILES - 1
-        halves = [slice(0, BANK), slice(BANK, S)]
+        stream = [kept("stream%d" % k, [P, S], F32) for k in range(STREAM_TILES)]
+        banks = [psum.tile([P, BANK], F32, name="bank%d" % k) for k in range(2 * PACK)]
         page = {}
-        z_bf = {}
+        z_woven = {}
+        y_woven = {}
 
         def static_products(i):
             rows = slice(P * i, P * (i + 1))
-            for h in range(2):
-                cols = slice(BANK * h, BANK * (h + 1))
+            for h, cols in enumerate(halves):
                 nc.tensor.matmul_mx(
                     out=banks[h][:], lhsT=w1_c[:, rows].bitcast(FP8X4), lhsT_scale=w1_s[:, rows],
                     rhs=v_w[:, cols].bitcast(FP8X4), rhs_scale=v_s[:, cols], start=True, stop=True,
@@ -171,119 +183,75 @@ def tile_list_woven_video_residual_kernel(
                     lhsT_scale=w23_s[:, rows],
                     rhs=v_w[:, cols].bitcast(FP8X4), rhs_scale=v_s[:, cols], start=True, stop=True,
                 )
-                nc.scalar.copy(first_sums[:, cols], banks[h][:])
+                nc.scalar.copy(w1_sums[:, cols], banks[h][:])
 
-        def static_lesser(i):
-            for h in range(2):
-                cols = slice(BANK * h, BANK * (h + 1))
-                nc.vector.tensor_tensor(stream[i % 3][:, cols], banks[2 + h][:], first_sums[:, cols], ALU.min)
-            nc.gpsimd.tensor_tensor(factor[i % 2][:], stream[i % 3][:], gate1[i % PACK], ALU.mult)
+        def static_values(i):
+            h1 = stream[i % STREAM_TILES]
+            for h, cols in enumerate(halves):
+                nc.vector.tensor_tensor(h1[:, cols], banks[2 + h][:], w1_sums[:, cols], ALU.min)
+            nc.gpsimd.tensor_tensor(factor[i % 2][:], h1[:], gate1[i % PACK], ALU.mult)
 
         def static_scatter(i):
-            page[i] = pages.tile([P, T2], F32, name="page%d" % i, tag="page")
+            page[i] = page_pool.tile([P, T2], F32, name="page%d" % i, tag="page")
             nc.vector.tensor_copy(page[i][:].indirect(idx3[:]), factor[i % 2][:])
 
         def moving_values(i):
             rows = slice(P * i, P * (i + 1))
-            response = stream[i % 3]
-            squared = squares
-            damping = first_sums if i == last else factor[i % 2]
-            for h in range(2):
-                cols = slice(BANK * h, BANK * (h + 1))
+            b = stream[i % STREAM_TILES]
+            damping = w1_sums if i == LAST else factor[i % 2]
+            for h, cols in enumerate(halves):
                 for a in range(2):
                     nc.tensor.matmul_mx(
                         out=banks[h][:], lhsT=w3_c[:, a, rows].bitcast(FP8X4), lhsT_scale=w23_s[4 + 4 * a :, rows],
                         rhs=v2_w[a][:, cols].bitcast(FP8X4), rhs_scale=v2_s[4 * a :, cols],
                         start=(a == 0), stop=(a == 1),
                     )
-                nc.scalar.copy(response[:, cols], banks[h][:])
+                nc.scalar.copy(b[:, cols], banks[h][:])
             for cols in halves:
-                nc.scalar.activation(squared[:, cols], response[:, cols], ACT.Square)
+                nc.scalar.activation(squares[:, cols], b[:, cols], ACT.Square)
             for cols in halves:
-                nc.scalar.activation(damping[:, cols], squared[:, cols], ACT.Abs_reciprocal_sqrt, bias=1.0)
+                nc.scalar.activation(damping[:, cols], squares[:, cols], ACT.Abs_reciprocal_sqrt, bias=1.0)
             for cols in halves:
                 nc.gpsimd.tensor_tensor(damping[:, cols], damping[:, cols], gate2[i % PACK][:, cols], ALU.mult)
             for cols in halves:
-                nc.gpsimd.tensor_tensor(response[:, cols], response[:, cols], damping[:, cols], ALU.mult)
+                nc.gpsimd.tensor_tensor(b[:, cols], b[:, cols], damping[:, cols], ALU.mult)
 
         def moving_scatter(i):
-            nc.vector.tensor_copy(page[i][:].indirect(idx4[:]), stream[i % 3][:])
+            nc.vector.tensor_copy(page[i][:].indirect(idx4[:]), stream[i % STREAM_TILES][:])
 
         def round_page(i):
             g, t = divmod(i, PACK)
-            nc.scalar.copy(squares[:, S - 1 : S], gains[:, g, t : t + 1])
+            nc.scalar.copy(gain_column, gains[:, g, t : t + 1])
             for c in range(CHUNKS):
                 if t == 0:
-                    z_bf[g, c] = woven.tile([P, BANK, PACK], BF16, name="z_bf%d_%d" % (g, c), tag="z_bf", align_bytes=64)
-                rows = page[i][:, BANK * c : BANK * (c + 1)]
-                if i == last and c < 1:
-                    nc.vector.tensor_scalar(z_bf[g, c][:, :, t], rows, squares[:, S - 1 : S], None, ALU.mult)
+                    z_woven[g, c] = woven("z_woven%d_%d" % (g, c), BANK)
+                page_chunk = page[i][:, BANK * c : BANK * (c + 1)]
+                if i == LAST and c == 0:
+                    nc.vector.tensor_scalar(z_woven[g, c][:, :, t], page_chunk, gain_column, None, ALU.mult)
                 else:
-                    nc.scalar.activation(z_bf[g, c][:, :, t], rows, ACT.Copy, scale=squares[:, S - 1 : S])
+                    nc.scalar.activation(z_woven[g, c][:, :, t], page_chunk, ACT.Copy, scale=gain_column)
 
         def quantize_z(g, c):
             cols = slice(BANK * c, BANK * (c + 1))
             nc.vector.quantize_mx(
                 out=z_c[:, g, cols].bitcast(FP8X4), scales=z_s[:, g, cols],
-                in_=z_bf[g, c][:].rearrange("p m t -> p (m t)"),
+                in_=z_woven[g, c][:].rearrange("p m t -> p (m t)"),
             )
 
         def y_bank(c, t):
             return banks[PACK * ((c + 1) % 2) + t]
 
-        def project(g, c):
+        def project(passes, c):
             cols = slice(BANK * c, BANK * (c + 1))
-            for t in range(PACK):
+            for t, g in itertools.product(range(PACK), passes):
                 rows = slice(P * t, P * (t + 1))
                 nc.tensor.matmul_mx(
                     out=y_bank(c, t)[:], lhsT=w4_c[:, g, rows].bitcast(FP8X4), lhsT_scale=w4_s[:, g, rows],
                     rhs=z_c[:, g, cols].bitcast(FP8X4), rhs_scale=z_s[:, g, cols], start=(g == 0), stop=(g == 1),
                 )
 
-        static_products(0)
-        nc.vector.tensor_copy(v2_w[0][:], tab2_w[0][:].indirect(idx2[:]))
-        static_lesser(0)
-        static_products(1)
-        nc.vector.tensor_copy(v2_w[1][:], tab2_w[1][:].indirect(idx2[:]))
-        nc.vector.tensor_copy(v2_s[:], tab2_s[:].indirect(idx2[:]))
-        nc.vector.tensor_copy(
-            w3_c[:].bitcast(I32).rearrange("p a c -> p (a c)").rearrange("p (g t m) -> p g m t", g=4, t=PACK),
-            w3_raw[:].bitcast(I32).rearrange("p a c -> p (a c)").rearrange("p (g m t) -> p g m t", g=4, t=PACK),
-        )
-        static_lesser(1)
-        static_scatter(0)
-        moving_values(0)
-        static_products(2)
-        quantize_weight("w1_dealt1", w1_raw1, w1_c[:, BANK:], w1_s[:, BANK:])
-        y = [load_rows("y%d" % c, up[:, BANK * c : BANK * (c + 1)]) for c in range(CHUNKS)]
-        for i in range(1, ROW_TILES):
-            static_scatter(i)
-            if i + 1 < ROW_TILES:
-                static_lesser(i + 1)
-            if i == PACK + 1:
-                for c in range(CHUNKS):
-                    quantize_z(0, c)
-                project(0, 0)
-            moving_scatter(i - 1)
-            if i < last:
-                moving_values(i)
-            if i + 2 < ROW_TILES:
-                static_products(i + 2)
-            if i in (3, 4):
-                g = i - 3
-                quantize_weight("w4_dealt%d" % g, w4_raw[g], w4_c[:, g, :], w4_s[:, g, :])
-            if i + 1 == last:
-                moving_values(last)
-            round_page(i - 1)
-        project(0, 1)
-        moving_scatter(last)
-        round_page(last)
-
         out_rows = out_0.rearrange("(p t) c -> p t c", t=PACK)
         out_words = out_1[0].rearrange("p m t -> p (m t)").bitcast(I32)
-
-        pieces = [(0, 0, 512), (1, 0, 512), (2, 0, 512), (3, 0, 256), (3, 256, 512)]
-        y_bf = {}
 
         def add_up(c, lo, hi):
             cols = slice(BANK * c + lo, BANK * c + hi)
@@ -291,34 +259,70 @@ def tile_list_woven_video_residual_kernel(
                 nc.vector.tensor_tensor(y[c][:, t, lo:hi], y_bank(c, t)[:, lo:hi], y[c][:, t, lo:hi], ALU.add)
                 if t % 2 == 1:
                     nc.sync.dma_start(out_rows[:, t - 1 : t + 1, cols], y[c][:, t - 1 : t + 1, lo:hi])
-            y_bf[c, lo] = woven.tile([P, hi - lo, PACK], BF16, name="y_bf%d_%d" % (c, lo), tag="z_bf", align_bytes=64)
+            y_woven[c, lo] = woven("y_woven%d_%d" % (c, lo), hi - lo)
             nc.scalar.copy(
-                y_bf[c, lo][:].rearrange("p (m i) t -> p m t i", i=4),
-                y[c][:, :, lo:hi].rearrange("p t (m i) -> p m t i", i=4),
+                y_woven[c, lo][:].rearrange("p (m e) t -> p m t e", e=LINE),
+                y[c][:, :, lo:hi].rearrange("p t (m e) -> p m t e", e=LINE),
             )
 
         def quantize_y(c, lo, hi):
             cols = slice(BANK * c + lo, BANK * c + hi)
             nc.vector.quantize_mx(
-                out=y_c[:, cols].bitcast(FP8X4), scales=y_s[:, cols], in_=y_bf[c, lo][:].rearrange("p m t -> p (m t)")
+                out=y_c[:, cols].bitcast(FP8X4), scales=y_s[:, cols],
+                in_=y_woven[c, lo][:].rearrange("p m t -> p (m t)"),
             )
             nc.sync.dma_start(out_words[:, cols], y_c[:, cols].bitcast(I32))
 
-        quantize_z(1, 0)
-        project(1, 0)
-        quantize_z(1, 1)
-        project(1, 1)
+        static_products(0)
+        nc.vector.tensor_copy(v2_w[0][:], tab2_w[0][:].indirect(idx2[:]))
+        static_values(0)
+        static_products(1)
+        nc.vector.tensor_copy(v2_w[1][:], tab2_w[1][:].indirect(idx2[:]))
+        nc.vector.tensor_copy(
+            w3_c[:].bitcast(I32).rearrange("p a c -> p (a c)").rearrange("p (u t m e) -> p u m t e", u=4, t=PACK, e=LINE),
+            w3_raw[:].bitcast(I32).rearrange("p a c -> p (a c)").rearrange("p (u m e t) -> p u m t e", u=4, t=PACK, e=LINE),
+        )
+        static_values(1)
+        static_scatter(0)
+        moving_values(0)
+        static_products(2)
+        quantize_weight("w1_dealt1", w1_raw[1], w1_c[:, BANK:], w1_s[:, BANK:])
+        y = [load_rows("y%d" % c, up[:, BANK * c : BANK * (c + 1)]) for c in range(CHUNKS)]
+
+        for i in range(1, ROW_TILES):
+            static_scatter(i)
+            if i < LAST:
+                static_values(i + 1)
+            if i == PACK + 1:
+                for c in range(CHUNKS):
+                    quantize_z(0, c)
+                project((0,), 0)
+            moving_scatter(i - 1)
+            if i < LAST:
+                moving_values(i)
+            if i + 2 <= LAST:
+                static_products(i + 2)
+            if i in (W4_STEP, W4_STEP + 1):
+                g = i - W4_STEP
+                quantize_weight("w4_dealt%d" % g, w4_raw[g], w4_c[:, g, :], w4_s[:, g, :])
+            if i + 1 == LAST:
+                moving_values(LAST)
+            round_page(i - 1)
+        project((0,), 1)
+        moving_scatter(LAST)
+        round_page(LAST)
+
+        for c in range(2):
+            quantize_z(1, c)
+            project((1,), c)
         for n, (c, lo, hi) in enumerate(pieces):
             add_up(c, lo, hi)
-            if c + 2 < CHUNKS and hi == BANK:
+            if c + 2 < CHUNKS:
                 quantize_z(1, c + 2)
-                project(0, c + 2)
-                project(1, c + 2)
-            if n >= 2:
-                quantize_y(*pieces[n - 2])
-        for piece in pieces[len(pieces) - 2 :]:
+                project((0, 1), c + 2)
+            if n >= Y_LAG:
+                quantize_y(*pieces[n - Y_LAG])
+        for piece in pieces[-Y_LAG:]:
             quantize_y(*piece)
-        for q in range(4):
-            nc.sync.dma_start(
-                out_2[0, 4 * q : 4 * q + 4, :].bitcast(I32), y_s[32 * q : 32 * q + 4, :].bitcast(I32)
-            )
+        for q in range(QUADRANTS):
+            nc.sync.dma_start(out_2[0, 4 * q : 4 * q + 4, :].bitcast(I32), y_s[32 * q : 32 * q + 4, :].bitcast(I32))

@@ -24,12 +24,13 @@ QUADRANTS = 4
 LINE = 4
 ROW_TILES = H // P
 LAST = ROW_TILES - 1
-CHUNKS = T2 // BANK
+PIECES = T2 // BANK + 1
 STAGE_SLOTS = 6
 PAGES = 3
 STREAM_TILES = 3
 W4_STEP = 3
-Y_LAG = 2
+Y_LAG = 3
+GPSIMD_PIECES = 2
 
 
 def tile_list_woven_video_residual_kernel(
@@ -38,13 +39,14 @@ def tile_list_woven_video_residual_kernel(
 ):
     nc = tc.nc
     halves = (slice(0, BANK), slice(BANK, S))
-    pieces = [(c, 0, BANK) for c in range(CHUNKS - 1)] + [(CHUNKS - 1, 0, BANK // 2), (CHUNKS - 1, BANK // 2, BANK)]
+    cuts = [0] + [BANK // 2 + BANK * c for c in range(PIECES - 1)] + [T2]
+    pieces = [slice(lo, hi) for lo, hi in zip(cuts, cuts[1:])]
     with ExitStack() as ctx:
         keep = ctx.enter_context(tc.tile_pool(name="keep", bufs=1))
         stage = ctx.enter_context(tc.tile_pool(name="stage", bufs=STAGE_SLOTS))
         dealt_pool = ctx.enter_context(tc.tile_pool(name="dealt", bufs=2))
         page_pool = ctx.enter_context(tc.tile_pool(name="pages", bufs=PAGES))
-        woven_pool = ctx.enter_context(tc.tile_pool(name="woven", bufs=CHUNKS))
+        woven_pool = ctx.enter_context(tc.tile_pool(name="woven", bufs=PIECES))
         psum = ctx.enter_context(tc.psum_pool(name="psum", bufs=1))
 
         def kept(name, shape, dtype):
@@ -74,7 +76,7 @@ def tile_list_woven_video_residual_kernel(
             return words
 
         def load_rows(name, src):
-            raw = staged(name, [P, PACK, BANK], F32)
+            raw = staged(name, [P, PACK, src.shape[1]], F32)
             nc.sync.dma_start(raw[:], src.rearrange("(p j) c -> p j c", j=PACK))
             return raw
 
@@ -134,12 +136,12 @@ def tile_list_woven_video_residual_kernel(
         w2_c = kept("w2_c", [P, 2 * H], U8)
         w23_s = kept("w23_s", [P, H], U8)
         nc.vector.tensor_copy(
-            w2_c[:].rearrange("p (g t m b) -> p g t m b", g=2, t=PACK, b=2),
-            w2_raw[:].rearrange("p (g m t b) -> p g t m b", g=2, t=PACK, b=2),
+            w2_c[:].bitcast(U16).rearrange("p (g t m) -> p g m t", g=2, t=PACK),
+            w2_raw[:].bitcast(U16).rearrange("p (g m t) -> p g m t", g=2, t=PACK),
         )
         nc.vector.tensor_copy(
-            w23_s[:].rearrange("p (g t m) -> p g t m", g=2, t=PACK),
-            w23_s_raw[:].rearrange("p (g m t) -> p g t m", g=2, t=PACK),
+            w23_s[:].rearrange("p (g t m) -> p g m t", g=2, t=PACK),
+            w23_s_raw[:].rearrange("p (g m t) -> p g m t", g=2, t=PACK),
         )
         w1_c = kept("w1_c", [P, H], U32)
         w1_s = kept("w1_s", [P, H], U8)
@@ -198,7 +200,7 @@ def tile_list_woven_video_residual_kernel(
         def moving_values(i):
             rows = slice(P * i, P * (i + 1))
             b = stream[i % STREAM_TILES]
-            damping = w1_sums if i == LAST else factor[i % 2]
+            damping = {0: stream[STREAM_TILES - 1], LAST: w1_sums}.get(i, factor[i % 2])
             for h, cols in enumerate(halves):
                 for a in range(2):
                     nc.tensor.matmul_mx(
@@ -222,54 +224,56 @@ def tile_list_woven_video_residual_kernel(
         def round_page(i):
             g, t = divmod(i, PACK)
             nc.scalar.copy(gain_column, gains[:, g, t : t + 1])
-            for c in range(CHUNKS):
+            for c, cols in enumerate(pieces):
                 if t == 0:
-                    z_woven[g, c] = woven("z_woven%d_%d" % (g, c), BANK)
-                page_chunk = page[i][:, BANK * c : BANK * (c + 1)]
+                    z_woven[g, c] = woven("z_woven%d_%d" % (g, c), cols.stop - cols.start)
+                page_piece = page[i][:, cols]
                 if i == LAST and c == 0:
-                    nc.vector.tensor_scalar(z_woven[g, c][:, :, t], page_chunk, gain_column, None, ALU.mult)
+                    nc.vector.tensor_scalar(z_woven[g, c][:, :, t], page_piece, gain_column, None, ALU.mult)
+                elif i == LAST - 1 and c >= PIECES - GPSIMD_PIECES:
+                    nc.gpsimd.tensor_scalar(z_woven[g, c][:, :, t], page_piece, gain_column, 0.0, ALU.mult, ALU.add)
                 else:
-                    nc.scalar.activation(z_woven[g, c][:, :, t], page_chunk, ACT.Copy, scale=gain_column)
+                    nc.scalar.activation(z_woven[g, c][:, :, t], page_piece, ACT.Copy, scale=gain_column)
 
         def quantize_z(g, c):
-            cols = slice(BANK * c, BANK * (c + 1))
+            cols = pieces[c]
             nc.vector.quantize_mx(
                 out=z_c[:, g, cols].bitcast(FP8X4), scales=z_s[:, g, cols],
                 in_=z_woven[g, c][:].rearrange("p m t -> p (m t)"),
             )
 
         def y_bank(c, t):
-            return banks[PACK * ((c + 1) % 2) + t]
+            return banks[PACK * ((c + 1) % 2) + t][:, 0 : pieces[c].stop - pieces[c].start]
 
         def project(passes, c):
-            cols = slice(BANK * c, BANK * (c + 1))
+            cols = pieces[c]
             for t, g in itertools.product(range(PACK), passes):
                 rows = slice(P * t, P * (t + 1))
                 nc.tensor.matmul_mx(
-                    out=y_bank(c, t)[:], lhsT=w4_c[:, g, rows].bitcast(FP8X4), lhsT_scale=w4_s[:, g, rows],
+                    out=y_bank(c, t), lhsT=w4_c[:, g, rows].bitcast(FP8X4), lhsT_scale=w4_s[:, g, rows],
                     rhs=z_c[:, g, cols].bitcast(FP8X4), rhs_scale=z_s[:, g, cols], start=(g == 0), stop=(g == 1),
                 )
 
         out_rows = out_0.rearrange("(p t) c -> p t c", t=PACK)
         out_words = out_1[0].rearrange("p m t -> p (m t)").bitcast(I32)
 
-        def add_up(c, lo, hi):
-            cols = slice(BANK * c + lo, BANK * c + hi)
+        def add_up(c):
+            cols = pieces[c]
             for t in range(PACK):
-                nc.vector.tensor_tensor(y[c][:, t, lo:hi], y_bank(c, t)[:, lo:hi], y[c][:, t, lo:hi], ALU.add)
+                nc.vector.tensor_tensor(y[c][:, t, :], y_bank(c, t), y[c][:, t, :], ALU.add)
                 if t % 2 == 1:
-                    nc.sync.dma_start(out_rows[:, t - 1 : t + 1, cols], y[c][:, t - 1 : t + 1, lo:hi])
-            y_woven[c, lo] = woven("y_woven%d_%d" % (c, lo), hi - lo)
+                    nc.sync.dma_start(out_rows[:, t - 1 : t + 1, cols], y[c][:, t - 1 : t + 1, :])
+            y_woven[c] = woven("y_woven%d" % c, cols.stop - cols.start)
             nc.scalar.copy(
-                y_woven[c, lo][:].rearrange("p (m e) t -> p m t e", e=LINE),
-                y[c][:, :, lo:hi].rearrange("p t (m e) -> p m t e", e=LINE),
+                y_woven[c][:].rearrange("p (m e) t -> p m t e", e=LINE),
+                y[c][:].rearrange("p t (m e) -> p m t e", e=LINE),
             )
 
-        def quantize_y(c, lo, hi):
-            cols = slice(BANK * c + lo, BANK * c + hi)
+        def quantize_y(c):
+            cols = pieces[c]
             nc.vector.quantize_mx(
                 out=y_c[:, cols].bitcast(FP8X4), scales=y_s[:, cols],
-                in_=y_woven[c, lo][:].rearrange("p m t -> p (m t)"),
+                in_=y_woven[c][:].rearrange("p m t -> p (m t)"),
             )
             nc.sync.dma_start(out_words[:, cols], y_c[:, cols].bitcast(I32))
 
@@ -287,14 +291,14 @@ def tile_list_woven_video_residual_kernel(
         moving_values(0)
         static_products(2)
         quantize_weight("w1_dealt1", w1_raw[1], w1_c[:, BANK:], w1_s[:, BANK:])
-        y = [load_rows("y%d" % c, up[:, BANK * c : BANK * (c + 1)]) for c in range(CHUNKS)]
+        y = [load_rows("y%d" % c, up[:, cols]) for c, cols in enumerate(pieces)]
 
         for i in range(1, ROW_TILES):
             static_scatter(i)
             if i < LAST:
                 static_values(i + 1)
             if i == PACK + 1:
-                for c in range(CHUNKS):
+                for c in range(PIECES):
                     quantize_z(0, c)
                 project((0,), 0)
             moving_scatter(i - 1)
@@ -315,14 +319,14 @@ def tile_list_woven_video_residual_kernel(
         for c in range(2):
             quantize_z(1, c)
             project((1,), c)
-        for n, (c, lo, hi) in enumerate(pieces):
-            add_up(c, lo, hi)
-            if c + 2 < CHUNKS:
+        for c in range(PIECES):
+            add_up(c)
+            if c + 2 < PIECES:
                 quantize_z(1, c + 2)
                 project((0, 1), c + 2)
-            if n >= Y_LAG:
-                quantize_y(*pieces[n - Y_LAG])
-        for piece in pieces[-Y_LAG:]:
-            quantize_y(*piece)
+            if c >= Y_LAG:
+                quantize_y(c - Y_LAG)
+        for c in range(PIECES - Y_LAG, PIECES):
+            quantize_y(c)
         for q in range(QUADRANTS):
             nc.sync.dma_start(out_2[0, 4 * q : 4 * q + 4, :].bitcast(I32), y_s[32 * q : 32 * q + 4, :].bitcast(I32))

@@ -29,6 +29,7 @@ STAGE_SLOTS = 6
 PAGES = 3
 STREAM_TILES = 3
 W4_STEP = 3
+Z_STEP = PACK + 2
 Y_LAG = 3
 GPSIMD_PIECES = 2
 
@@ -44,13 +45,17 @@ def tile_list_woven_video_residual_kernel(
     with ExitStack() as ctx:
         keep = ctx.enter_context(tc.tile_pool(name="keep", bufs=1))
         stage = ctx.enter_context(tc.tile_pool(name="stage", bufs=STAGE_SLOTS))
-        dealt_pool = ctx.enter_context(tc.tile_pool(name="dealt", bufs=2))
+        dealt_pool = ctx.enter_context(tc.tile_pool(name="dealt", bufs=1))
         page_pool = ctx.enter_context(tc.tile_pool(name="pages", bufs=PAGES))
         woven_pool = ctx.enter_context(tc.tile_pool(name="woven", bufs=PIECES))
+        shared = ctx.enter_context(tc.tile_pool(name="shared", bufs=1))
         psum = ctx.enter_context(tc.psum_pool(name="psum", bufs=1))
 
         def kept(name, shape, dtype):
             return keep.tile(shape, dtype, name=name, align_bytes=64)
+
+        def placed(name, shape, dtype, offset):
+            return shared.tile(shape, dtype, name=name, align_bytes=64, offset=offset)
 
         def staged(name, shape, dtype):
             return stage.tile(shape, dtype, name=name, tag="stage", align_bytes=64)
@@ -88,13 +93,14 @@ def tile_list_woven_video_residual_kernel(
             for t in range(t0, t1):
                 gate[t] = tile[:, t - t0, :]
 
-        def quantize_weight(name, raw, codes, scales):
-            dealt = dealt_pool.tile([P, BANK * PACK], BF16, name=name, tag="dealt", align_bytes=64)
+        def dealt(name):
+            return dealt_pool.tile([P, 2, BANK * PACK], BF16, name=name, tag="dealt", align_bytes=64)
+
+        def deal_weight(half, raw):
             nc.scalar.copy(
-                dealt[:].rearrange("p (t m j) -> p m t j", t=PACK, j=PACK),
+                half.rearrange("p (t m j) -> p m t j", t=PACK, j=PACK),
                 raw[:].rearrange("p j (m t) -> p m t j", t=PACK),
             )
-            nc.vector.quantize_mx(out=codes.bitcast(FP8X4), scales=scales, in_=dealt[:])
 
         tab_s = kept("tab_s", [P, T], U8)
         tab2_s = kept("tab2_s", [P, T], U8)
@@ -144,8 +150,10 @@ def tile_list_woven_video_residual_kernel(
             w23_s_raw[:].rearrange("p (g m t) -> p g m t", g=2, t=PACK),
         )
         w1_c = kept("w1_c", [P, H], U32)
-        w1_s = kept("w1_s", [P, H], U8)
-        quantize_weight("w1_dealt0", w1_raw[0], w1_c[:, 0:BANK], w1_s[:, 0:BANK])
+        w1_s = {0: kept("w1_s0", [P, BANK], U8)}
+        w1_dealt = dealt("w1_dealt")
+        deal_weight(w1_dealt[:, 0, :], w1_raw[0])
+        nc.vector.quantize_mx(out=w1_c[:, 0:BANK].bitcast(FP8X4), scales=w1_s[0][:], in_=w1_dealt[:, 0, :])
 
         gains = kept("gains", [P, 2, PACK], F32)
         nc.sync.dma_start(gains[:], gain.rearrange("(g p t) -> p g t", g=2, t=PACK))
@@ -157,16 +165,16 @@ def tile_list_woven_video_residual_kernel(
         v2_w = [kept("v2_w%d" % a, [P, S], U32) for a in range(2)]
         w3_c = kept("w3_c", [P, 2, H], U32)
         w4_c = kept("w4_c", [P, 2, N], U32)
-        w4_s = kept("w4_s", [P, 2, N], U8)
         z_c = kept("z_c", [P, 2, T2], U32)
-        z_s = kept("z_s", [P, 2, T2], U8)
+        z_s = {1: kept("z_s1", [P, T2], U8)}
         y_c = kept("y_c", [P, T2], U32)
         y_s = kept("y_s", [P, T2], U8)
 
         squares = kept("squares", [P, S], F32)
         gain_column = squares[:, S - 1 : S]
         w1_sums = kept("w1_sums", [P, S], F32)
-        factor = [kept("factor%d" % k, [P, S], F32) for k in range(2)]
+        factor_start = [0, 4 * S + BANK + T2]
+        factor = [placed("factor%d" % k, [P, S], F32, factor_start[k]) for k in range(2)]
         stream = [kept("stream%d" % k, [P, S], F32) for k in range(STREAM_TILES)]
         banks = [psum.tile([P, BANK], F32, name="bank%d" % k) for k in range(2 * PACK)]
         page = {}
@@ -174,10 +182,11 @@ def tile_list_woven_video_residual_kernel(
         y_woven = {}
 
         def static_products(i):
+            g, t = divmod(i, PACK)
             rows = slice(P * i, P * (i + 1))
             for h, cols in enumerate(halves):
                 nc.tensor.matmul_mx(
-                    out=banks[h][:], lhsT=w1_c[:, rows].bitcast(FP8X4), lhsT_scale=w1_s[:, rows],
+                    out=banks[h][:], lhsT=w1_c[:, rows].bitcast(FP8X4), lhsT_scale=w1_s[g][:, P * t : P * (t + 1)],
                     rhs=v_w[:, cols].bitcast(FP8X4), rhs_scale=v_s[:, cols], start=True, stop=True,
                 )
                 nc.tensor.matmul_mx(
@@ -196,6 +205,13 @@ def tile_list_woven_video_residual_kernel(
         def static_scatter(i):
             page[i] = page_pool.tile([P, T2], F32, name="page%d" % i, tag="page")
             nc.vector.tensor_copy(page[i][:].indirect(idx3[:]), factor[i % 2][:])
+
+        def scales_after_scatter(name, i, size):
+            start = factor_start[i % 2]
+            scales = placed(name, [P, size], U8, start)
+            factor_start[i % 2] = start + size
+            factor[i % 2] = placed("factor_above_%s" % name, [P, S], F32, start + size)
+            return scales
 
         def moving_values(i):
             rows = slice(P * i, P * (i + 1))
@@ -238,7 +254,7 @@ def tile_list_woven_video_residual_kernel(
         def quantize_z(g, c):
             cols = pieces[c]
             nc.vector.quantize_mx(
-                out=z_c[:, g, cols].bitcast(FP8X4), scales=z_s[:, g, cols],
+                out=z_c[:, g, cols].bitcast(FP8X4), scales=z_s[g][:, cols],
                 in_=z_woven[g, c][:].rearrange("p m t -> p (m t)"),
             )
 
@@ -248,10 +264,10 @@ def tile_list_woven_video_residual_kernel(
         def project(passes, c):
             cols = pieces[c]
             for t, g in itertools.product(range(PACK), passes):
-                rows = slice(P * t, P * (t + 1))
                 nc.tensor.matmul_mx(
-                    out=y_bank(c, t), lhsT=w4_c[:, g, rows].bitcast(FP8X4), lhsT_scale=w4_s[:, g, rows],
-                    rhs=z_c[:, g, cols].bitcast(FP8X4), rhs_scale=z_s[:, g, cols], start=(g == 0), stop=(g == 1),
+                    out=y_bank(c, t), lhsT=w4_c[:, g, P * t : P * (t + 1)].bitcast(FP8X4),
+                    lhsT_scale=w4_s[:, N * g + P * t : N * g + P * (t + 1)],
+                    rhs=z_c[:, g, cols].bitcast(FP8X4), rhs_scale=z_s[g][:, cols], start=(g == 0), stop=(g == 1),
                 )
 
         out_rows = out_0.rearrange("(p t) c -> p t c", t=PACK)
@@ -282,36 +298,51 @@ def tile_list_woven_video_residual_kernel(
         static_values(0)
         static_products(1)
         nc.vector.tensor_copy(v2_w[1][:], tab2_w[1][:].indirect(idx2[:]))
+        w3_dealt_words = w3_c[:].bitcast(I32).rearrange("p a c -> p (a c)")
+        w3_raw_words = w3_raw[:].bitcast(I32).rearrange("p a c -> p (a c)")
         nc.vector.tensor_copy(
-            w3_c[:].bitcast(I32).rearrange("p a c -> p (a c)").rearrange("p (u t m e) -> p u m t e", u=4, t=PACK, e=LINE),
-            w3_raw[:].bitcast(I32).rearrange("p a c -> p (a c)").rearrange("p (u m e t) -> p u m t e", u=4, t=PACK, e=LINE),
+            w3_dealt_words.rearrange("p (u t m e) -> p u m t e", u=4, t=PACK, e=LINE),
+            w3_raw_words.rearrange("p (u m e t) -> p u m t e", u=4, t=PACK, e=LINE),
         )
         static_values(1)
         static_scatter(0)
         moving_values(0)
         static_products(2)
-        quantize_weight("w1_dealt1", w1_raw[1], w1_c[:, BANK:], w1_s[:, BANK:])
+        deal_weight(w1_dealt[:, 1, :], w1_raw[1])
         y = [load_rows("y%d" % c, up[:, cols]) for c, cols in enumerate(pieces)]
 
         for i in range(1, ROW_TILES):
             static_scatter(i)
-            if i < LAST:
-                static_values(i + 1)
-            if i == PACK + 1:
+            if i + 2 == PACK:
+                w1_s[1] = scales_after_scatter("w1_s1", i, BANK)
+                nc.vector.quantize_mx(out=w1_c[:, BANK:].bitcast(FP8X4), scales=w1_s[1][:], in_=w1_dealt[:, 1, :])
+            if i == W4_STEP + 2:
+                w4_s = scales_after_scatter("w4_s", i, 2 * N)
+                nc.vector.quantize_mx(
+                    out=w4_c[:].rearrange("p g n -> p (g n)").bitcast(FP8X4), scales=w4_s[:],
+                    in_=w4_dealt[:].rearrange("p g n -> p (g n)"),
+                )
+            if i == Z_STEP:
+                z_s[0] = scales_after_scatter("z_s0", i, T2)
                 for c in range(PIECES):
                     quantize_z(0, c)
                 project((0,), 0)
+                round_page(PACK)
+            if i < LAST:
+                static_values(i + 1)
             moving_scatter(i - 1)
             if i < LAST:
                 moving_values(i)
             if i + 2 <= LAST:
                 static_products(i + 2)
+            if i == W4_STEP:
+                w4_dealt = dealt("w4_dealt")
             if i in (W4_STEP, W4_STEP + 1):
-                g = i - W4_STEP
-                quantize_weight("w4_dealt%d" % g, w4_raw[g], w4_c[:, g, :], w4_s[:, g, :])
+                deal_weight(w4_dealt[:, i - W4_STEP, :], w4_raw[i - W4_STEP])
             if i + 1 == LAST:
                 moving_values(LAST)
-            round_page(i - 1)
+            if i - 1 != PACK:
+                round_page(i - 1)
         project((0,), 1)
         moving_scatter(LAST)
         round_page(LAST)

@@ -122,9 +122,9 @@ def tile_list_woven_video_residual_kernel(
         load_scale_rows(w23_s_raw, 0, w2_scales)
         tab2_w = [load_table_words("tab2_w0", tab2_words[0])]
         load_scale_rows(w23_s_raw, 4, w3_scales)
-        tab2_w.append(load_table_words("tab2_w1", tab2_words[1]))
         w3_raw = staged("w3_raw", [P, 2, H], U32)
         nc.sync.dma_start(w3_raw[:].bitcast(I32), w3_words.rearrange("a p c i -> p a (c i)").bitcast(I32))
+        tab2_w.append(load_table_words("tab2_w1", tab2_words[1]))
         idx3 = load_list("idx3", offs3)
         load_gate(gate1, "gate1", wg1, 0, 1)
         load_gate(gate1, "gate1", wg1, 1, 2)
@@ -295,15 +295,15 @@ def tile_list_woven_video_residual_kernel(
 
         static_products(0)
         nc.vector.tensor_copy(v2_w[0][:], tab2_w[0][:].indirect(idx2[:]))
-        static_values(0)
-        static_products(1)
-        nc.vector.tensor_copy(v2_w[1][:], tab2_w[1][:].indirect(idx2[:]))
         w3_dealt_words = w3_c[:].bitcast(I32).rearrange("p a c -> p (a c)")
         w3_raw_words = w3_raw[:].bitcast(I32).rearrange("p a c -> p (a c)")
         nc.vector.tensor_copy(
             w3_dealt_words.rearrange("p (u t m e) -> p u m t e", u=4, t=PACK, e=LINE),
             w3_raw_words.rearrange("p (u m e t) -> p u m t e", u=4, t=PACK, e=LINE),
         )
+        static_values(0)
+        static_products(1)
+        nc.vector.tensor_copy(v2_w[1][:], tab2_w[1][:].indirect(idx2[:]))
         static_values(1)
         static_scatter(0)
         moving_values(0)

@@ -29,8 +29,10 @@ STAGE_SLOTS = 6
 PAGES = 3
 STREAM_TILES = 3
 W4_STEP = 3
-Z_STEP = PACK + 2
 Y_LAG = 3
+STREAM_AT = 2 * 4 * S + BANK + 2 * N
+W3_AT = STREAM_AT + STREAM_TILES * 4 * S
+DEALT_AT = W3_AT + 2 * 4 * H
 GPSIMD_PIECES = 2
 
 
@@ -45,9 +47,8 @@ def tile_list_woven_video_residual_kernel(
     with ExitStack() as ctx:
         keep = ctx.enter_context(tc.tile_pool(name="keep", bufs=1))
         stage = ctx.enter_context(tc.tile_pool(name="stage", bufs=STAGE_SLOTS))
-        dealt_pool = ctx.enter_context(tc.tile_pool(name="dealt", bufs=1))
         page_pool = ctx.enter_context(tc.tile_pool(name="pages", bufs=PAGES))
-        woven_pool = ctx.enter_context(tc.tile_pool(name="woven", bufs=PIECES))
+        woven_pool = ctx.enter_context(tc.tile_pool(name="woven", bufs=2))
         shared = ctx.enter_context(tc.tile_pool(name="shared", bufs=1))
         psum = ctx.enter_context(tc.psum_pool(name="psum", bufs=1))
 
@@ -60,8 +61,9 @@ def tile_list_woven_video_residual_kernel(
         def staged(name, shape, dtype):
             return stage.tile(shape, dtype, name=name, tag="stage", align_bytes=64)
 
-        def woven(name, columns):
-            return woven_pool.tile([P, columns, PACK], BF16, name=name, tag="woven", align_bytes=64)
+        def woven(name, c):
+            columns = pieces[c].stop - pieces[c].start
+            return woven_pool.tile([P, columns, PACK], BF16, name=name, tag="woven%d" % c, align_bytes=64)
 
         def load_list(name, src):
             offsets = keep.tile([P, S // 16], U16, name=name)
@@ -94,7 +96,7 @@ def tile_list_woven_video_residual_kernel(
                 gate[t] = tile[:, t - t0, :]
 
         def dealt(name):
-            return dealt_pool.tile([P, 2, BANK * PACK], BF16, name=name, tag="dealt", align_bytes=64)
+            return placed(name, [P, 2, BANK * PACK], BF16, DEALT_AT)
 
         def deal_weight(half, raw):
             nc.scalar.copy(
@@ -157,25 +159,23 @@ def tile_list_woven_video_residual_kernel(
 
         gains = kept("gains", [P, 2, PACK], F32)
         nc.sync.dma_start(gains[:], gain.rearrange("(g p t) -> p g t", g=2, t=PACK))
-        load_gate(gate2, "gate2", wg2, 1, 2)
         load_gate(gate1, "gate1", wg1, 2, PACK)
+        load_gate(gate2, "gate2", wg2, 1, 2)
         load_gate(gate2, "gate2", wg2, 2, PACK)
         w4_raw = [load_rows("w4_raw%d" % g, w4[BANK * g : BANK * (g + 1), :]) for g in range(2)]
 
         v2_w = [kept("v2_w%d" % a, [P, S], U32) for a in range(2)]
-        w3_c = kept("w3_c", [P, 2, H], U32)
+        w3_c = placed("w3_c", [P, 2, H], U32, W3_AT)
         w4_c = kept("w4_c", [P, 2, N], U32)
-        z_c = kept("z_c", [P, 2, T2], U32)
-        z_s = {1: kept("z_s1", [P, T2], U8)}
         y_c = kept("y_c", [P, T2], U32)
         y_s = kept("y_s", [P, T2], U8)
 
         squares = kept("squares", [P, S], F32)
         gain_column = squares[:, S - 1 : S]
         w1_sums = kept("w1_sums", [P, S], F32)
-        factor_start = [0, 4 * S + BANK + T2]
+        factor_start = [0, 4 * S + BANK]
         factor = [placed("factor%d" % k, [P, S], F32, factor_start[k]) for k in range(2)]
-        stream = [kept("stream%d" % k, [P, S], F32) for k in range(STREAM_TILES)]
+        stream = [placed("stream%d" % k, [P, S], F32, STREAM_AT + 4 * S * k) for k in range(STREAM_TILES)]
         banks = [psum.tile([P, BANK], F32, name="bank%d" % k) for k in range(2 * PACK)]
         page = {}
         z_woven = {}
@@ -229,10 +229,15 @@ def tile_list_woven_video_residual_kernel(
                 nc.scalar.activation(squares[:, cols], b[:, cols], ACT.Square)
             for cols in halves:
                 nc.scalar.activation(damping[:, cols], squares[:, cols], ACT.Abs_reciprocal_sqrt, bias=1.0)
+            return damping
+
+        def moving_gate(i, damping):
+            b = stream[i % STREAM_TILES]
+            gated = factor[i % 2] if i in (0, LAST) else stream[(i - 1) % STREAM_TILES]
             for cols in halves:
-                nc.gpsimd.tensor_tensor(damping[:, cols], damping[:, cols], gate2[i % PACK][:, cols], ALU.mult)
+                nc.gpsimd.tensor_tensor(gated[:, cols], damping[:, cols], gate2[i % PACK][:, cols], ALU.mult)
             for cols in halves:
-                nc.gpsimd.tensor_tensor(b[:, cols], b[:, cols], damping[:, cols], ALU.mult)
+                nc.gpsimd.tensor_tensor(b[:, cols], b[:, cols], gated[:, cols], ALU.mult)
 
         def moving_scatter(i):
             nc.vector.tensor_copy(page[i][:].indirect(idx4[:]), stream[i % STREAM_TILES][:])
@@ -242,11 +247,9 @@ def tile_list_woven_video_residual_kernel(
             nc.scalar.copy(gain_column, gains[:, g, t : t + 1])
             for c, cols in enumerate(pieces):
                 if t == 0:
-                    z_woven[g, c] = woven("z_woven%d_%d" % (g, c), cols.stop - cols.start)
+                    z_woven[g, c] = woven("z_woven%d_%d" % (g, c), c)
                 page_piece = page[i][:, cols]
-                if i == LAST and c == 0:
-                    nc.vector.tensor_scalar(z_woven[g, c][:, :, t], page_piece, gain_column, None, ALU.mult)
-                elif i == LAST - 1 and c >= PIECES - GPSIMD_PIECES:
+                if i == LAST - 1 and c >= PIECES - GPSIMD_PIECES:
                     nc.gpsimd.tensor_scalar(z_woven[g, c][:, :, t], page_piece, gain_column, 0.0, ALU.mult, ALU.add)
                 else:
                     nc.scalar.activation(z_woven[g, c][:, :, t], page_piece, ACT.Copy, scale=gain_column)
@@ -254,20 +257,20 @@ def tile_list_woven_video_residual_kernel(
         def quantize_z(g, c):
             cols = pieces[c]
             nc.vector.quantize_mx(
-                out=z_c[:, g, cols].bitcast(FP8X4), scales=z_s[g][:, cols],
+                out=z_c[g][:, cols].bitcast(FP8X4), scales=z_s[g][:, cols],
                 in_=z_woven[g, c][:].rearrange("p m t -> p (m t)"),
             )
 
         def y_bank(c, t):
             return banks[PACK * ((c + 1) % 2) + t][:, 0 : pieces[c].stop - pieces[c].start]
 
-        def project(passes, c):
+        def project(c):
             cols = pieces[c]
-            for t, g in itertools.product(range(PACK), passes):
+            for g, t in itertools.product(range(2), range(PACK)):
                 nc.tensor.matmul_mx(
                     out=y_bank(c, t), lhsT=w4_c[:, g, P * t : P * (t + 1)].bitcast(FP8X4),
                     lhsT_scale=w4_s[:, N * g + P * t : N * g + P * (t + 1)],
-                    rhs=z_c[:, g, cols].bitcast(FP8X4), rhs_scale=z_s[g][:, cols], start=(g == 0), stop=(g == 1),
+                    rhs=z_c[g][:, cols].bitcast(FP8X4), rhs_scale=z_s[g][:, cols], start=(g == 0), stop=(g == 1),
                 )
 
         out_rows = out_0.rearrange("(p t) c -> p t c", t=PACK)
@@ -279,7 +282,7 @@ def tile_list_woven_video_residual_kernel(
                 nc.vector.tensor_tensor(y[c][:, t, :], y_bank(c, t), y[c][:, t, :], ALU.add)
                 if t % 2 == 1:
                     nc.sync.dma_start(out_rows[:, t - 1 : t + 1, cols], y[c][:, t - 1 : t + 1, :])
-            y_woven[c] = woven("y_woven%d" % c, cols.stop - cols.start)
+            y_woven[c] = woven("y_woven%d" % c, c)
             nc.scalar.copy(
                 y_woven[c][:].rearrange("p (m e) t -> p m t e", e=LINE),
                 y[c][:].rearrange("p t (m e) -> p m t e", e=LINE),
@@ -306,13 +309,15 @@ def tile_list_woven_video_residual_kernel(
         nc.vector.tensor_copy(v2_w[1][:], tab2_w[1][:].indirect(idx2[:]))
         static_values(1)
         static_scatter(0)
-        moving_values(0)
+        moving_gate(0, moving_values(0))
         static_products(2)
         deal_weight(w1_dealt[:, 1, :], w1_raw[1])
         y = [load_rows("y%d" % c, up[:, cols]) for c, cols in enumerate(pieces)]
 
         for i in range(1, ROW_TILES):
             static_scatter(i)
+            if i == LAST:
+                moving_gate(LAST, last_damping)
             if i + 2 == PACK:
                 w1_s[1] = scales_after_scatter("w1_s1", i, BANK)
                 nc.vector.quantize_mx(out=w1_c[:, BANK:].bitcast(FP8X4), scales=w1_s[1][:], in_=w1_dealt[:, 1, :])
@@ -322,17 +327,11 @@ def tile_list_woven_video_residual_kernel(
                     out=w4_c[:].rearrange("p g n -> p (g n)").bitcast(FP8X4), scales=w4_s[:],
                     in_=w4_dealt[:].rearrange("p g n -> p (g n)"),
                 )
-            if i == Z_STEP:
-                z_s[0] = scales_after_scatter("z_s0", i, T2)
-                for c in range(PIECES):
-                    quantize_z(0, c)
-                project((0,), 0)
-                round_page(PACK)
             if i < LAST:
                 static_values(i + 1)
             moving_scatter(i - 1)
             if i < LAST:
-                moving_values(i)
+                moving_gate(i, moving_values(i))
             if i + 2 <= LAST:
                 static_products(i + 2)
             if i == W4_STEP:
@@ -340,21 +339,26 @@ def tile_list_woven_video_residual_kernel(
             if i in (W4_STEP, W4_STEP + 1):
                 deal_weight(w4_dealt[:, i - W4_STEP, :], w4_raw[i - W4_STEP])
             if i + 1 == LAST:
-                moving_values(LAST)
-            if i - 1 != PACK:
-                round_page(i - 1)
-        project((0,), 1)
+                last_damping = moving_values(LAST)
+            round_page(i - 1)
         moving_scatter(LAST)
         round_page(LAST)
 
+        z_c = [placed("z_c%d" % g, [P, T2], U32, at) for g, at in enumerate((W3_AT, DEALT_AT))]
+        last_stream_at = STREAM_AT + 4 * S * (LAST % STREAM_TILES)
+        z_s = [placed("z_s%d" % g, [P, T2], U8, last_stream_at + T2 * g) for g in range(2)]
         for c in range(2):
+            quantize_z(0, 2 * c)
+            quantize_z(0, 2 * c + 1)
             quantize_z(1, c)
-            project((1,), c)
+            project(c)
         for c in range(PIECES):
             add_up(c)
+            if c == 0:
+                quantize_z(0, PIECES - 1)
             if c + 2 < PIECES:
                 quantize_z(1, c + 2)
-                project((0, 1), c + 2)
+                project(c + 2)
             if c >= Y_LAG:
                 quantize_y(c - Y_LAG)
         for c in range(PIECES - Y_LAG, PIECES):

@@ -21,6 +21,7 @@ P = 128
 PACK = 4
 BANK = 512
 QUADRANTS = 4
+BY_HALVES = (0, 2, 1, 3)
 LINE = 4
 ROW_TILES = H // P
 LAST = ROW_TILES - 1
@@ -70,12 +71,12 @@ def tile_list_woven_video_residual_kernel(
             nc.sync.dma_start(offsets[:], src)
             return offsets
 
-        def load_scale_rows(dst, first, src):
+        def load_scale_rows(queue, dst, first, src):
             passes = src.shape[0]
             for q in range(QUADRANTS):
                 start = 32 * q + first
                 scale_rows = src[:, 4 * q : 4 * q + 4, :] if passes > 1 else src[0, 4 * q : 4 * q + 4, :]
-                nc.sync.dma_start(dst[start : start + 4 * passes, :].bitcast(I32), scale_rows.bitcast(I32))
+                queue.dma_start(dst[start : start + 4 * passes, :].bitcast(I32), scale_rows.bitcast(I32))
 
         def load_table_words(name, src):
             words = staged(name, [P, T], U32)
@@ -90,7 +91,7 @@ def tile_list_woven_video_residual_kernel(
         def load_gate(gate, name, src, t0, t1):
             by_slot = src.rearrange("(p t) j -> p t j", t=PACK)
             tile = kept("%s_%d" % (name, t0), [P, t1 - t0, S], F32)
-            for q in range(QUADRANTS):
+            for q in BY_HALVES:
                 nc.sync.dma_start(tile[32 * q : 32 * q + 32, :, :], by_slot[:, t0:t1, :])
             for t in range(t0, t1):
                 gate[t] = tile[:, t - t0, :]
@@ -117,13 +118,13 @@ def tile_list_woven_video_residual_kernel(
         idx = load_list("idx", offs)
         idx2 = load_list("idx2", offs2)
         nc.sync.dma_start(w2_raw[:].bitcast(I32), w2_words[0].bitcast(I32))
-        load_scale_rows(tab_s, 0, tab_scales)
+        load_scale_rows(nc.sync, tab_s, 0, tab_scales)
         tab_w = load_table_words("tab_w", tab_words[0])
-        load_scale_rows(tab2_s, 0, tab2_scales)
+        load_scale_rows(nc.sync, tab2_s, 0, tab2_scales)
         w1_raw = [load_rows("w1_raw0", w1[:, 0:BANK])]
-        load_scale_rows(w23_s_raw, 0, w2_scales)
+        load_scale_rows(nc.sync, w23_s_raw, 0, w2_scales)
         tab2_w = [load_table_words("tab2_w0", tab2_words[0])]
-        load_scale_rows(w23_s_raw, 4, w3_scales)
+        load_scale_rows(nc.gpsimd, w23_s_raw, 4, w3_scales)
         w3_raw = staged("w3_raw", [P, 2, H], U32)
         nc.sync.dma_start(w3_raw[:].bitcast(I32), w3_words.rearrange("a p c i -> p a (c i)").bitcast(I32))
         tab2_w.append(load_table_words("tab2_w1", tab2_words[1]))

@@ -120,8 +120,8 @@ def tile_list_woven_video_residual_kernel(
         nc.sync.dma_start(w2_raw[:].bitcast(I32), w2_words[0].bitcast(I32))
         load_scale_rows(nc.sync, tab_s, 0, tab_scales)
         tab_w = load_table_words("tab_w", tab_words[0])
-        load_scale_rows(nc.sync, tab2_s, 0, tab2_scales)
         w1_raw = [load_rows("w1_raw0", w1[:, 0:BANK])]
+        load_scale_rows(nc.sync, tab2_s, 0, tab2_scales)
         load_scale_rows(nc.sync, w23_s_raw, 0, w2_scales)
         tab2_w = [load_table_words("tab2_w0", tab2_words[0])]
         load_scale_rows(nc.gpsimd, w23_s_raw, 4, w3_scales)
@@ -138,9 +138,9 @@ def tile_list_woven_video_residual_kernel(
         v_s = kept("v_s", [P, S], U8)
         v_w = kept("v_w", [P, S], U32)
         nc.vector.tensor_copy(v_s[:], tab_s[:].indirect(idx[:]))
+        nc.vector.tensor_copy(v_w[:], tab_w[:].indirect(idx[:]))
         v2_s = kept("v2_s", [P, S], U8)
         nc.vector.tensor_copy(v2_s[:], tab2_s[:].indirect(idx2[:]))
-        nc.vector.tensor_copy(v_w[:], tab_w[:].indirect(idx[:]))
 
         w2_c = kept("w2_c", [P, 2 * H], U8)
         w23_s = kept("w23_s", [P, H], U8)

@@ -299,9 +299,9 @@ def tile_list_woven_video_residual_kernel(
 
         static_products(0)
         nc.vector.tensor_copy(v2_w[0][:], tab2_w[0][:].indirect(idx2[:]))
-        w3_dealt_words = w3_c[:].bitcast(I32).rearrange("p a c -> p (a c)")
-        w3_raw_words = w3_raw[:].bitcast(I32).rearrange("p a c -> p (a c)")
-        nc.vector.tensor_copy(
+        w3_dealt_words = w3_c[:].rearrange("p a c -> p (a c)")
+        w3_raw_words = w3_raw[:].rearrange("p a c -> p (a c)")
+        nc.scalar.copy(
             w3_dealt_words.rearrange("p (u t m e) -> p u m t e", u=4, t=PACK, e=LINE),
             w3_raw_words.rearrange("p (u m e t) -> p u m t e", u=4, t=PACK, e=LINE),
         )

@@ -198,7 +198,7 @@ def tile_list_woven_video_residual_kernel(
                 nc.scalar.copy(w1_sums[:, cols], banks[h][:])
 
         def static_values(i):
-            h1 = stream[i % STREAM_TILES]
+            h1 = stream[i % 2]
             for h, cols in enumerate(halves):
                 nc.vector.tensor_tensor(h1[:, cols], banks[2 + h][:], w1_sums[:, cols], ALU.min)
             nc.gpsimd.tensor_tensor(factor[i % 2][:], h1[:], gate1[i % PACK], ALU.mult)
@@ -216,7 +216,7 @@ def tile_list_woven_video_residual_kernel(
 
         def moving_values(i):
             rows = slice(P * i, P * (i + 1))
-            b = stream[i % STREAM_TILES]
+            b = stream[i % 2]
             damping = {0: stream[STREAM_TILES - 1], LAST: w1_sums}.get(i, factor[i % 2])
             for h, cols in enumerate(halves):
                 for a in range(2):
@@ -232,16 +232,19 @@ def tile_list_woven_video_residual_kernel(
                 nc.scalar.activation(damping[:, cols], squares[:, cols], ACT.Abs_reciprocal_sqrt, bias=1.0)
             return damping
 
+        def gated_h2(i):
+            return stream[i % 2 if i == LAST else STREAM_TILES - 1]
+
         def moving_gate(i, damping):
-            b = stream[i % STREAM_TILES]
-            gated = factor[i % 2] if i in (0, LAST) else stream[(i - 1) % STREAM_TILES]
+            b = stream[i % 2]
+            gated = factor[i % 2] if i in (0, LAST) else stream[(i + 1) % 2]
             for cols in halves:
                 nc.gpsimd.tensor_tensor(gated[:, cols], damping[:, cols], gate2[i % PACK][:, cols], ALU.mult)
             for cols in halves:
-                nc.gpsimd.tensor_tensor(b[:, cols], b[:, cols], gated[:, cols], ALU.mult)
+                nc.gpsimd.tensor_tensor(gated_h2(i)[:, cols], b[:, cols], gated[:, cols], ALU.mult)
 
         def moving_scatter(i):
-            nc.vector.tensor_copy(page[i][:].indirect(idx4[:]), stream[i % STREAM_TILES][:])
+            nc.vector.tensor_copy(page[i][:].indirect(idx4[:]), gated_h2(i)[:])
 
         def round_page(i):
             g, t = divmod(i, PACK)
@@ -346,7 +349,7 @@ def tile_list_woven_video_residual_kernel(
         round_page(LAST)
 
         z_c = [placed("z_c%d" % g, [P, T2], U32, at) for g, at in enumerate((W3_AT, DEALT_AT))]
-        last_stream_at = STREAM_AT + 4 * S * (LAST % STREAM_TILES)
+        last_stream_at = STREAM_AT + 4 * S * (LAST % 2)
         z_s = [placed("z_s%d" % g, [P, T2], U8, last_stream_at + T2 * g) for g in range(2)]
         for c in range(2):
             quantize_z(0, 2 * c)

@@ -1,4 +1,3 @@
-import itertools
 from contextlib import ExitStack
 
 import concourse.mybir as mybir
@@ -25,16 +24,19 @@ BY_HALVES = (0, 2, 1, 3)
 LINE = 4
 ROW_TILES = H // P
 LAST = ROW_TILES - 1
-PIECES = T2 // BANK + 1
-STAGE_SLOTS = 6
-PAGES = 3
-STREAM_TILES = 3
-W4_STEP = 3
+WIDTHS = (256, 512, 512, 512, 256)
 Y_LAG = 3
-STREAM_AT = 2 * 4 * S + BANK + 2 * N
-W3_AT = STREAM_AT + STREAM_TILES * 4 * S
-DEALT_AT = W3_AT + 2 * 4 * H
-GPSIMD_PIECES = 2
+KB = 1024
+
+UP_AT = 0
+WOVEN_AT = (32 * KB, 48 * KB)
+PAIRS_AT = 64 * KB
+V2_AT = 80 * KB
+W3_AT = 88 * KB
+W2_AT = 96 * KB
+STATIC_AT = 98 * KB
+MOVING_AT = 102 * KB
+PAGE_AT = 110 * KB
 
 
 def tile_list_woven_video_residual_kernel(
@@ -43,13 +45,10 @@ def tile_list_woven_video_residual_kernel(
 ):
     nc = tc.nc
     halves = (slice(0, BANK), slice(BANK, S))
-    cuts = [0] + [BANK // 2 + BANK * c for c in range(PIECES - 1)] + [T2]
+    cuts = [sum(WIDTHS[:c]) for c in range(len(WIDTHS) + 1)]
     pieces = [slice(lo, hi) for lo, hi in zip(cuts, cuts[1:])]
     with ExitStack() as ctx:
         keep = ctx.enter_context(tc.tile_pool(name="keep", bufs=1))
-        stage = ctx.enter_context(tc.tile_pool(name="stage", bufs=STAGE_SLOTS))
-        page_pool = ctx.enter_context(tc.tile_pool(name="pages", bufs=PAGES))
-        woven_pool = ctx.enter_context(tc.tile_pool(name="woven", bufs=2))
         shared = ctx.enter_context(tc.tile_pool(name="shared", bufs=1))
         psum = ctx.enter_context(tc.psum_pool(name="psum", bufs=1))
 
@@ -59,223 +58,222 @@ def tile_list_woven_video_residual_kernel(
         def placed(name, shape, dtype, offset):
             return shared.tile(shape, dtype, name=name, align_bytes=64, offset=offset)
 
-        def staged(name, shape, dtype):
-            return stage.tile(shape, dtype, name=name, tag="stage", align_bytes=64)
-
-        def woven(name, c):
-            columns = pieces[c].stop - pieces[c].start
-            return woven_pool.tile([P, columns, PACK], BF16, name=name, tag="woven%d" % c, align_bytes=64)
-
         def load_list(name, src):
             offsets = keep.tile([P, S // 16], U16, name=name)
             nc.sync.dma_start(offsets[:], src)
             return offsets
 
-        def load_scale_rows(queue, dst, first, src):
+        def load_scale_rows(queue, dst, src):
             passes = src.shape[0]
             for q in range(QUADRANTS):
-                start = 32 * q + first
                 scale_rows = src[:, 4 * q : 4 * q + 4, :] if passes > 1 else src[0, 4 * q : 4 * q + 4, :]
-                queue.dma_start(dst[start : start + 4 * passes, :].bitcast(I32), scale_rows.bitcast(I32))
+                queue.dma_start(dst[32 * q : 32 * q + 4 * passes, :].bitcast(I32), scale_rows.bitcast(I32))
 
-        def load_table_words(name, src):
-            words = staged(name, [P, T], U32)
+        def load_words(name, src, offset):
+            words = placed(name, [P, T], U32, offset)
             nc.sync.dma_start(words[:].bitcast(I32), src.rearrange("p t i -> p (t i)").bitcast(I32))
             return words
 
-        def load_rows(name, src):
-            raw = staged(name, [P, PACK, src.shape[1]], F32)
+        def load_rows(name, src, offset):
+            raw = placed(name, [P, PACK, src.shape[1]], F32, offset)
             nc.sync.dma_start(raw[:], src.rearrange("(p j) c -> p j c", j=PACK))
             return raw
 
-        def load_gate(gate, name, src, t0, t1):
-            by_slot = src.rearrange("(p t) j -> p t j", t=PACK)
-            tile = kept("%s_%d" % (name, t0), [P, t1 - t0, S], F32)
+        def load_gate(name, src, t):
+            by_slot = src.rearrange("(i t e) j -> t i e j", t=PACK, e=2)
+            tile = kept("%s_%d" % (name, t), [P, S], F32)
             for q in BY_HALVES:
-                nc.sync.dma_start(tile[32 * q : 32 * q + 32, :, :], by_slot[:, t0:t1, :])
-            for t in range(t0, t1):
-                gate[t] = tile[:, t - t0, :]
+                nc.sync.dma_start(tile[32 * q : 32 * q + 32, :], by_slot[t])
+            return tile
 
-        def dealt(name):
-            return placed(name, [P, 2, BANK * PACK], BF16, DEALT_AT)
-
-        def deal_weight(half, raw):
-            nc.scalar.copy(
-                half.rearrange("p (t m j) -> p m t j", t=PACK, j=PACK),
-                raw[:].rearrange("p j (m t) -> p m t j", t=PACK),
-            )
-
-        tab_s = kept("tab_s", [P, T], U8)
-        tab2_s = kept("tab2_s", [P, T], U8)
-        w23_s_raw = kept("w23_s_raw", [P, H], U8)
-        nc.vector.memset(tab_s[:].bitcast(I32), 0)
-        nc.vector.memset(tab2_s[:].bitcast(I32), 0)
-        nc.vector.memset(w23_s_raw[:].bitcast(I32), 0)
+        small_at = WOVEN_AT[1] + 8 * KB
+        w2_raw = placed("w2_raw", [P, 2 * H], U8, small_at)
+        tab_s = placed("tab_s", [P, T], U8, small_at + 2 * KB)
+        tab2_s = placed("tab2_s", [P, T], U8, small_at + 4 * KB)
+        w2_s_raw = placed("w2_s_raw", [P, H], U8, small_at + 6 * KB)
+        w3_s_raw = placed("w3_s_raw", [P, H], U8, small_at + 7 * KB)
+        for scale_tile in (tab_s, tab2_s, w2_s_raw, w3_s_raw):
+            nc.vector.memset(scale_tile[:].bitcast(I32), 0)
 
         gate1 = {}
         gate2 = {}
-        w2_raw = kept("w2_raw", [P, 2 * H], U8)
         idx = load_list("idx", offs)
         idx2 = load_list("idx2", offs2)
         nc.sync.dma_start(w2_raw[:].bitcast(I32), w2_words[0].bitcast(I32))
-        load_scale_rows(nc.sync, tab_s, 0, tab_scales)
-        tab_w = load_table_words("tab_w", tab_words[0])
-        w1_raw = [load_rows("w1_raw0", w1[:, 0:BANK])]
-        load_scale_rows(nc.sync, tab2_s, 0, tab2_scales)
-        load_scale_rows(nc.sync, w23_s_raw, 0, w2_scales)
-        tab2_w = [load_table_words("tab2_w0", tab2_words[0])]
-        load_scale_rows(nc.gpsimd, w23_s_raw, 4, w3_scales)
-        w3_raw = staged("w3_raw", [P, 2, H], U32)
-        nc.sync.dma_start(w3_raw[:].bitcast(I32), w3_words.rearrange("a p c i -> p a (c i)").bitcast(I32))
-        tab2_w.append(load_table_words("tab2_w1", tab2_words[1]))
+        load_scale_rows(nc.sync, tab_s, tab_scales)
+        tab_w = load_words("tab_w", tab_words[0], UP_AT)
+        load_scale_rows(nc.sync, tab2_s, tab2_scales)
+        w1_raw = [load_rows("w1_raw0", w1[:, 0:BANK], WOVEN_AT[0])]
+        load_scale_rows(nc.sync, w2_s_raw, w2_scales)
+        tab2_w = [load_words("tab2_w0", tab2_words[0], UP_AT + 8 * KB)]
         idx3 = load_list("idx3", offs3)
-        load_gate(gate1, "gate1", wg1, 0, 1)
-        load_gate(gate1, "gate1", wg1, 1, 2)
+        gate1[0] = load_gate("gate1", wg1, 0)
+        tab2_w.append(load_words("tab2_w1", tab2_words[1], PAGE_AT))
+        w3_raw = placed("w3_raw", [P, 2, H], U32, UP_AT + 24 * KB)
+        nc.sync.dma_start(w3_raw[:].bitcast(I32), w3_words.rearrange("a p c i -> p a (c i)").bitcast(I32))
+        load_scale_rows(nc.sync, w3_s_raw, w3_scales)
+        gate1[1] = load_gate("gate1", wg1, 1)
         idx4 = load_list("idx4", offs4)
-        load_gate(gate2, "gate2", wg2, 0, 1)
-        w1_raw.append(load_rows("w1_raw1", w1[:, BANK : 2 * BANK]))
+        gate2[0] = load_gate("gate2", wg2, 0)
+        w1_raw.append(load_rows("w1_raw1", w1[:, BANK : 2 * BANK], WOVEN_AT[0] + 8 * KB))
+        gate1[2] = load_gate("gate1", wg1, 2)
+        gains = [kept("gains%d" % g, [P, PACK], F32) for g in range(2)]
+        with nc.allow_non_contiguous_dma(reason="the four gains of a partition lie two elements apart"):
+            for g in range(2):
+                for e in range(2):
+                    nc.sync.dma_start(gains[g][e:P:2, :], gain.rearrange("(g i t e) -> g e i t", g=2, t=PACK, e=2)[g, e])
+        gate2[1] = load_gate("gate2", wg2, 1)
+        gate1[3] = load_gate("gate1", wg1, 3)
+        gate2[2] = load_gate("gate2", wg2, 2)
+        gate2[3] = load_gate("gate2", wg2, 3)
 
         v_s = kept("v_s", [P, S], U8)
         v_w = kept("v_w", [P, S], U32)
-        nc.vector.tensor_copy(v_s[:], tab_s[:].indirect(idx[:]))
-        nc.vector.tensor_copy(v_w[:], tab_w[:].indirect(idx[:]))
         v2_s = kept("v2_s", [P, S], U8)
-        nc.vector.tensor_copy(v2_s[:], tab2_s[:].indirect(idx2[:]))
-
-        w2_c = kept("w2_c", [P, 2 * H], U8)
-        w23_s = kept("w23_s", [P, H], U8)
-        nc.vector.tensor_copy(
-            w2_c[:].bitcast(U16).rearrange("p (g t m) -> p g m t", g=2, t=PACK),
-            w2_raw[:].bitcast(U16).rearrange("p (g m t) -> p g m t", g=2, t=PACK),
-        )
-        nc.vector.tensor_copy(
-            w23_s[:].rearrange("p (g t m) -> p g m t", g=2, t=PACK),
-            w23_s_raw[:].rearrange("p (g m t) -> p g m t", g=2, t=PACK),
-        )
-        w1_c = kept("w1_c", [P, H], U32)
-        w1_s = {0: kept("w1_s0", [P, BANK], U8)}
-        w1_dealt = dealt("w1_dealt")
-        deal_weight(w1_dealt[:, 0, :], w1_raw[0])
-        nc.vector.quantize_mx(out=w1_c[:, 0:BANK].bitcast(FP8X4), scales=w1_s[0][:], in_=w1_dealt[:, 0, :])
-
-        gains = kept("gains", [P, 2, PACK], F32)
-        nc.sync.dma_start(gains[:], gain.rearrange("(g p t) -> p g t", g=2, t=PACK))
-        load_gate(gate1, "gate1", wg1, 2, PACK)
-        load_gate(gate2, "gate2", wg2, 1, 2)
-        load_gate(gate2, "gate2", wg2, 2, PACK)
-        w4_raw = [load_rows("w4_raw%d" % g, w4[BANK * g : BANK * (g + 1), :]) for g in range(2)]
-
-        v2_w = [kept("v2_w%d" % a, [P, S], U32) for a in range(2)]
+        first_sums = placed("first_sums", [P, S], F32, V2_AT + 4 * KB)
+        v2_w = [placed("v2_w%d" % a, [P, S], U32, V2_AT + 4 * KB * a) for a in range(2)]
+        w2_c = placed("w2_c", [P, 2 * H], U8, W2_AT)
+        w2_s = kept("w2_s", [P, H], U8)
         w3_c = placed("w3_c", [P, 2, H], U32, W3_AT)
+        w3_s = kept("w3_s", [P, H], U8)
+        first_squares = placed("first_squares", [P, S], F32, WOVEN_AT[1] + 4 * KB)
+        w1_dealt = [placed("w1_dealt%d" % g, [P, BANK * PACK], BF16, WOVEN_AT[1] + 4 * KB * g) for g in range(2)]
+        w1_c = {}
+        w1_s = {}
+        w4_dealt = kept("w4_dealt", [P, 2, N * PACK], BF16)
         w4_c = kept("w4_c", [P, 2, N], U32)
         y_c = kept("y_c", [P, T2], U32)
         y_s = kept("y_s", [P, T2], U8)
+        lesser = [kept("lesser%d" % k, [P, S], F32) for k in range(2)]
+        factor = [kept("factor%d" % k, [P, S], F32) for k in range(2)]
+        first_gated = [placed("first_gated0", [P, S], F32, PAIRS_AT), placed("first_gated1", [P, S], F32, STATIC_AT)]
+        moving = [placed("moving%d" % k, [P, S], F32, MOVING_AT + 4 * KB * k) for k in range(2)]
 
-        squares = kept("squares", [P, S], F32)
-        gain_column = squares[:, S - 1 : S]
-        w1_sums = kept("w1_sums", [P, S], F32)
-        factor_start = [0, 4 * S + BANK]
-        factor = [placed("factor%d" % k, [P, S], F32, factor_start[k]) for k in range(2)]
-        stream = [placed("stream%d" % k, [P, S], F32, STREAM_AT + 4 * S * k) for k in range(STREAM_TILES)]
+        first_lesser = [placed("first_lesser%d" % k, [P, S], F32, UP_AT + 8 * KB + 4 * KB * k) for k in range(2)]
+
+        def first_bank(i):
+            return PACK if i == 1 else 0
+
+        def h1_of(i):
+            return first_lesser[i] if i < 2 else lesser[i % 2]
+
+        def w1_sums(i):
+            return {0: first_sums, 1: lesser[1]}.get(i, h1_of(i - 1))
+
+        def gated_h1(i):
+            return first_gated[i] if i < 2 else factor[i % 2]
         banks = [psum.tile([P, BANK], F32, name="bank%d" % k) for k in range(2 * PACK)]
         page = {}
+        pairs = {}
         z_woven = {}
         y_woven = {}
 
+        def deal_pairs(dst, src, dtype):
+            nc.scalar.copy(
+                dst.bitcast(dtype).rearrange("p (g t i) -> p g i t", g=2, t=PACK),
+                src.bitcast(dtype).rearrange("p (g i t) -> p g i t", g=2, t=PACK),
+            )
+
+        def deal_w1(g):
+            nc.scalar.copy(
+                w1_dealt[g][:].rearrange("p (t i e j) -> p i t j e", t=PACK, e=2, j=PACK),
+                w1_raw[g][:].rearrange("p j (i t e) -> p i t j e", t=PACK, e=2),
+            )
+
+        def quantize_w1(g):
+            nc.vector.quantize_mx(out=w1_c[g][:].bitcast(FP8X4), scales=w1_s[g][:], in_=w1_dealt[g][:])
+
         def static_products(i):
             g, t = divmod(i, PACK)
-            rows = slice(P * i, P * (i + 1))
+            first = first_bank(i)
             for h, cols in enumerate(halves):
                 nc.tensor.matmul_mx(
-                    out=banks[h][:], lhsT=w1_c[:, rows].bitcast(FP8X4), lhsT_scale=w1_s[g][:, P * t : P * (t + 1)],
+                    out=banks[first + h][:], lhsT=w1_c[g][:, P * t : P * (t + 1)].bitcast(FP8X4),
+                    lhsT_scale=w1_s[g][:, P * t : P * (t + 1)],
                     rhs=v_w[:, cols].bitcast(FP8X4), rhs_scale=v_s[:, cols], start=True, stop=True,
                 )
+            for h, cols in enumerate(halves):
                 nc.tensor.matmul_mx(
-                    out=banks[2 + h][:], lhsT=w2_c[:, 2 * P * i : 2 * P * (i + 1)].bitcast(FP4X4),
-                    lhsT_scale=w23_s[:, rows],
+                    out=banks[first + 2 + h][:], lhsT=w2_c[:, 2 * P * i : 2 * P * (i + 1)].bitcast(FP4X4),
+                    lhsT_scale=w2_s[:, P * i : P * (i + 1)],
                     rhs=v_w[:, cols].bitcast(FP8X4), rhs_scale=v_s[:, cols], start=True, stop=True,
                 )
-                nc.scalar.copy(w1_sums[:, cols], banks[h][:])
+            for h, cols in enumerate(halves):
+                nc.scalar.copy(w1_sums(i)[:, cols], banks[first + h][:])
 
         def static_values(i):
-            h1 = stream[i % 2]
+            h1 = h1_of(i)
             for h, cols in enumerate(halves):
-                nc.vector.tensor_tensor(h1[:, cols], banks[2 + h][:], w1_sums[:, cols], ALU.min)
-            nc.gpsimd.tensor_tensor(factor[i % 2][:], h1[:], gate1[i % PACK], ALU.mult)
+                nc.vector.tensor_tensor(h1[:, cols], banks[first_bank(i) + 2 + h][:], w1_sums(i)[:, cols], ALU.min)
+            nc.gpsimd.tensor_tensor(gated_h1(i)[:], h1[:], gate1[i % PACK][:], ALU.mult)
 
         def static_scatter(i):
-            page[i] = page_pool.tile([P, T2], F32, name="page%d" % i, tag="page")
-            nc.vector.tensor_copy(page[i][:].indirect(idx3[:]), factor[i % 2][:])
-
-        def scales_after_scatter(name, i, size):
-            start = factor_start[i % 2]
-            scales = placed(name, [P, size], U8, start)
-            factor_start[i % 2] = start + size
-            factor[i % 2] = placed("factor_above_%s" % name, [P, S], F32, start + size)
-            return scales
+            page[i] = placed("page%d" % i, [P, T2], F32, PAGE_AT + 8 * KB * (i % 3))
+            nc.vector.tensor_copy(page[i][:].indirect(idx3[:]), gated_h1(i)[:])
 
         def moving_values(i):
             rows = slice(P * i, P * (i + 1))
-            b = stream[i % 2]
-            damping = {0: stream[STREAM_TILES - 1], LAST: w1_sums}.get(i, factor[i % 2])
+            b = moving[i % 2]
+            damp = lesser[0] if i == LAST else factor[i % 2]
+            squares = first_squares if i == 0 else damp
             for h, cols in enumerate(halves):
                 for a in range(2):
                     nc.tensor.matmul_mx(
-                        out=banks[h][:], lhsT=w3_c[:, a, rows].bitcast(FP8X4), lhsT_scale=w23_s[4 + 4 * a :, rows],
+                        out=banks[4 + h][:], lhsT=w3_c[:, a, rows].bitcast(FP8X4), lhsT_scale=w3_s[4 * a :, rows],
                         rhs=v2_w[a][:, cols].bitcast(FP8X4), rhs_scale=v2_s[4 * a :, cols],
                         start=(a == 0), stop=(a == 1),
                     )
-                nc.scalar.copy(b[:, cols], banks[h][:])
+            for h, cols in enumerate(halves):
+                nc.scalar.copy(b[:, cols], banks[4 + h][:])
+            for h, cols in enumerate(halves):
+                nc.scalar.activation(squares[:, cols], banks[4 + h][:], ACT.Square)
             for cols in halves:
-                nc.scalar.activation(squares[:, cols], b[:, cols], ACT.Square)
-            for cols in halves:
-                nc.scalar.activation(damping[:, cols], squares[:, cols], ACT.Abs_reciprocal_sqrt, bias=1.0)
-            return damping
-
-        def gated_h2(i):
-            return stream[i % 2 if i == LAST else STREAM_TILES - 1]
-
-        def moving_gate(i, damping):
-            b = stream[i % 2]
-            gated = factor[i % 2] if i in (0, LAST) else stream[(i + 1) % 2]
-            for cols in halves:
-                nc.gpsimd.tensor_tensor(gated[:, cols], damping[:, cols], gate2[i % PACK][:, cols], ALU.mult)
-            for cols in halves:
-                nc.gpsimd.tensor_tensor(gated_h2(i)[:, cols], b[:, cols], gated[:, cols], ALU.mult)
+                nc.scalar.activation(damp[:, cols], squares[:, cols], ACT.Abs_reciprocal_sqrt, bias=1.0)
+            nc.gpsimd.tensor_tensor(b[:], b[:], gate2[i % PACK][:], ALU.mult)
+            nc.gpsimd.tensor_tensor(b[:], b[:], damp[:], ALU.mult)
 
         def moving_scatter(i):
-            nc.vector.tensor_copy(page[i][:].indirect(idx4[:]), gated_h2(i)[:])
+            nc.vector.tensor_copy(page[i][:].indirect(idx4[:]), moving[i % 2][:])
 
-        def round_page(i):
+        def round_piece(i, c):
             g, t = divmod(i, PACK)
-            nc.scalar.copy(gain_column, gains[:, g, t : t + 1])
-            for c, cols in enumerate(pieces):
-                if t == 0:
-                    z_woven[g, c] = woven("z_woven%d_%d" % (g, c), c)
-                page_piece = page[i][:, cols]
-                if i == LAST - 1 and c >= PIECES - GPSIMD_PIECES:
-                    nc.gpsimd.tensor_scalar(z_woven[g, c][:, :, t], page_piece, gain_column, 0.0, ALU.mult, ALU.add)
-                else:
-                    nc.scalar.activation(z_woven[g, c][:, :, t], page_piece, ACT.Copy, scale=gain_column)
+            cols = pieces[c]
+            if t == 0:
+                pairs[g, c] = placed("pairs%d_%d" % (g, c), [P, 2, WIDTHS[c], 2], BF16, PAIRS_AT + 8 * cols.start)
+            nc.scalar.activation(
+                pairs[g, c][:, t // 2, :, t % 2], page[i][:, cols], ACT.Copy, scale=gains[g][:, t : t + 1]
+            )
+
+        def weave_piece(g, c):
+            cols = pieces[c]
+            z_woven[g, c] = placed("z_woven%d_%d" % (g, c), [P, WIDTHS[c] * PACK], BF16, WOVEN_AT[g] + 8 * cols.start)
+            nc.scalar.copy(
+                z_woven[g, c][:].bitcast(U32).rearrange("p (m u) -> p m u", u=2),
+                pairs[g, c][:].rearrange("p u m e -> p (u m e)").bitcast(U32).rearrange("p (u m) -> p m u", u=2),
+            )
+
+        def deal_w4(g):
+            nc.scalar.copy(
+                w4_dealt[:, g, :].rearrange("p (t m j) -> p m t j", t=PACK, j=PACK),
+                w4_raw[g][:].rearrange("p j (m t) -> p m t j", t=PACK),
+            )
 
         def quantize_z(g, c):
             cols = pieces[c]
-            nc.vector.quantize_mx(
-                out=z_c[g][:, cols].bitcast(FP8X4), scales=z_s[g][:, cols],
-                in_=z_woven[g, c][:].rearrange("p m t -> p (m t)"),
-            )
+            nc.vector.quantize_mx(out=z_c[g][:, cols].bitcast(FP8X4), scales=z_s[g][:, cols], in_=z_woven[g, c][:])
 
         def y_bank(c, t):
-            return banks[PACK * ((c + 1) % 2) + t][:, 0 : pieces[c].stop - pieces[c].start]
+            return banks[PACK * ((c + 1) % 2) + t][:, 0 : WIDTHS[c]]
 
         def project(c):
             cols = pieces[c]
-            for g, t in itertools.product(range(2), range(PACK)):
-                nc.tensor.matmul_mx(
-                    out=y_bank(c, t), lhsT=w4_c[:, g, P * t : P * (t + 1)].bitcast(FP8X4),
-                    lhsT_scale=w4_s[:, N * g + P * t : N * g + P * (t + 1)],
-                    rhs=z_c[g][:, cols].bitcast(FP8X4), rhs_scale=z_s[g][:, cols], start=(g == 0), stop=(g == 1),
-                )
+            for g in range(2):
+                for t in range(PACK):
+                    nc.tensor.matmul_mx(
+                        out=y_bank(c, t), lhsT=w4_c[:, g, P * t : P * (t + 1)].bitcast(FP8X4),
+                        lhsT_scale=w4_s[:, N * g + P * t : N * g + P * (t + 1)],
+                        rhs=z_c[g][:, cols].bitcast(FP8X4), rhs_scale=z_s[g][:, cols], start=(g == 0), stop=(g == 1),
+                    )
 
         out_rows = out_0.rearrange("(p t) c -> p t c", t=PACK)
         out_words = out_1[0].rearrange("p m t -> p (m t)").bitcast(I32)
@@ -286,86 +284,103 @@ def tile_list_woven_video_residual_kernel(
                 nc.vector.tensor_tensor(y[c][:, t, :], y_bank(c, t), y[c][:, t, :], ALU.add)
                 if t % 2 == 1:
                     nc.sync.dma_start(out_rows[:, t - 1 : t + 1, cols], y[c][:, t - 1 : t + 1, :])
-            y_woven[c] = woven("y_woven%d" % c, c)
+            y_woven[c] = placed("y_woven%d" % c, [P, WIDTHS[c] * PACK], BF16, WOVEN_AT[0] + 8 * cols.start)
             nc.scalar.copy(
-                y_woven[c][:].rearrange("p (m e) t -> p m t e", e=LINE),
+                y_woven[c][:].rearrange("p (m e t) -> p m t e", e=LINE, t=PACK),
                 y[c][:].rearrange("p t (m e) -> p m t e", e=LINE),
             )
 
         def quantize_y(c):
             cols = pieces[c]
-            nc.vector.quantize_mx(
-                out=y_c[:, cols].bitcast(FP8X4), scales=y_s[:, cols],
-                in_=y_woven[c][:].rearrange("p m t -> p (m t)"),
-            )
+            nc.vector.quantize_mx(out=y_c[:, cols].bitcast(FP8X4), scales=y_s[:, cols], in_=y_woven[c][:])
             nc.sync.dma_start(out_words[:, cols], y_c[:, cols].bitcast(I32))
 
+        nc.vector.tensor_copy(v_s[:], tab_s[:].indirect(idx[:]))
+        nc.vector.tensor_copy(v_w[:], tab_w[:].indirect(idx[:]))
+        deal_pairs(w2_c[:], w2_raw[:], U32)
+        deal_w1(0)
+        deal_pairs(w2_s[:], w2_s_raw[:], U16)
+        w1_c[0] = kept("w1_c0", [P, BANK], U32)
+        w1_s[0] = kept("w1_s0", [P, BANK], U8)
+        quantize_w1(0)
+        nc.vector.tensor_copy(v2_s[:], tab2_s[:].indirect(idx2[:]))
         static_products(0)
         nc.vector.tensor_copy(v2_w[0][:], tab2_w[0][:].indirect(idx2[:]))
-        w3_dealt_words = w3_c[:].rearrange("p a c -> p (a c)")
-        w3_raw_words = w3_raw[:].rearrange("p a c -> p (a c)")
-        nc.scalar.copy(
-            w3_dealt_words.rearrange("p (u t m e) -> p u m t e", u=4, t=PACK, e=LINE),
-            w3_raw_words.rearrange("p (u m e t) -> p u m t e", u=4, t=PACK, e=LINE),
-        )
         static_values(0)
         static_products(1)
         nc.vector.tensor_copy(v2_w[1][:], tab2_w[1][:].indirect(idx2[:]))
         static_values(1)
+        nc.scalar.copy(
+            w3_c[:].rearrange("p a c -> p (a c)").rearrange("p (u t i e) -> p u i t e", u=4, t=PACK, e=2),
+            w3_raw[:].rearrange("p a c -> p (a c)").rearrange("p (u i t e) -> p u i t e", u=4, t=PACK, e=2),
+        )
+        deal_pairs(w3_s[:], w3_s_raw[:], U16)
         static_scatter(0)
-        moving_gate(0, moving_values(0))
+        moving_values(0)
+        deal_w1(1)
         static_products(2)
-        deal_weight(w1_dealt[:, 1, :], w1_raw[1])
-        y = [load_rows("y%d" % c, up[:, cols]) for c, cols in enumerate(pieces)]
+        w4_raw = [placed("w4_raw%d" % g, [P, PACK, N], F32, WOVEN_AT[1] + 8 * KB * (1 - g)) for g in range(2)]
+        w4_rows = w4.rearrange("(g i t e) n -> g t i e n", g=2, t=PACK, e=2)
+        for g in range(2):
+            for t in range(PACK):
+                nc.sync.dma_start(w4_raw[g][:, t, :], w4_rows[g, t])
+        y = [load_rows("y%d" % c, up[:, cols], UP_AT + 16 * cols.start) for c, cols in enumerate(pieces)]
 
         for i in range(1, ROW_TILES):
             static_scatter(i)
-            if i == LAST:
-                moving_gate(LAST, last_damping)
-            if i + 2 == PACK:
-                w1_s[1] = scales_after_scatter("w1_s1", i, BANK)
-                nc.vector.quantize_mx(out=w1_c[:, BANK:].bitcast(FP8X4), scales=w1_s[1][:], in_=w1_dealt[:, 1, :])
-            if i == W4_STEP + 2:
-                w4_s = scales_after_scatter("w4_s", i, 2 * N)
-                nc.vector.quantize_mx(
-                    out=w4_c[:].rearrange("p g n -> p (g n)").bitcast(FP8X4), scales=w4_s[:],
-                    in_=w4_dealt[:].rearrange("p g n -> p (g n)"),
-                )
+            if i == 1:
+                w1_c[1] = placed("w1_c1", [P, BANK], U32, STATIC_AT)
+                w1_s[1] = placed("w1_s1", [P, BANK], U8, STATIC_AT + 2 * KB)
+                quantize_w1(1)
             if i < LAST:
                 static_values(i + 1)
-            moving_scatter(i - 1)
+            if i == LAST:
+                moving_values(LAST)
+            if i >= 2:
+                for c in range(len(pieces)):
+                    round_piece(i - 2, c)
             if i < LAST:
-                moving_gate(i, moving_values(i))
+                moving_values(i)
+            moving_scatter(i - 1)
             if i + 2 <= LAST:
                 static_products(i + 2)
-            if i == W4_STEP:
-                w4_dealt = dealt("w4_dealt")
-            if i in (W4_STEP, W4_STEP + 1):
-                deal_weight(w4_dealt[:, i - W4_STEP, :], w4_raw[i - W4_STEP])
-            if i + 1 == LAST:
-                last_damping = moving_values(LAST)
-            round_page(i - 1)
+            if i in (2, 3):
+                deal_w4(i - 2)
+            if i - 2 == PACK - 1:
+                for c in range(len(pieces)):
+                    weave_piece(0, c)
+        for c in range(len(pieces)):
+            round_piece(LAST - 1, c)
         moving_scatter(LAST)
-        round_page(LAST)
 
-        z_c = [placed("z_c%d" % g, [P, T2], U32, at) for g, at in enumerate((W3_AT, DEALT_AT))]
-        last_stream_at = STREAM_AT + 4 * S * (LAST % 2)
-        z_s = [placed("z_s%d" % g, [P, T2], U8, last_stream_at + T2 * g) for g in range(2)]
-        for c in range(2):
-            quantize_z(0, 2 * c)
-            quantize_z(0, 2 * c + 1)
-            quantize_z(1, c)
-            project(c)
-        for c in range(PIECES):
+        last_at = MOVING_AT + 4 * KB * (LAST % 2)
+        w4_s = placed("w4_s", [P, 2 * N], U8, last_at)
+        z_c = [placed("z_c%d" % g, [P, T2], U32, at) for g, at in enumerate((W3_AT, V2_AT))]
+        z_s = [placed("z_s%d" % g, [P, T2], U8, at) for g, at in enumerate((last_at + 2 * N, W2_AT))]
+        nc.vector.quantize_mx(
+            out=w4_c[:].rearrange("p g n -> p (g n)").bitcast(FP8X4), scales=w4_s[:],
+            in_=w4_dealt[:].rearrange("p g n -> p (g n)"),
+        )
+        for c in range(len(pieces)):
+            round_piece(LAST, c)
+            weave_piece(1, c)
+        quantize_z(0, 0)
+        quantize_z(1, 0)
+        project(0)
+        quantize_z(0, 1)
+        quantize_z(0, 2)
+        quantize_z(1, 1)
+        project(1)
+        quantize_z(0, 3)
+        quantize_z(0, 4)
+        for c in range(len(pieces)):
             add_up(c)
-            if c == 0:
-                quantize_z(0, PIECES - 1)
-            if c + 2 < PIECES:
+            if c + 2 < len(pieces):
                 quantize_z(1, c + 2)
                 project(c + 2)
             if c >= Y_LAG:
                 quantize_y(c - Y_LAG)
-        for c in range(PIECES - Y_LAG, PIECES):
+        for c in range(len(pieces) - Y_LAG, len(pieces)):
             quantize_y(c)
         for q in range(QUADRANTS):
             nc.sync.dma_start(out_2[0, 4 * q : 4 * q + 4, :].bitcast(I32), y_s[32 * q : 32 * q + 4, :].bitcast(I32))

@@ -37,6 +37,7 @@ W2_AT = 96 * KB
 STATIC_AT = 98 * KB
 MOVING_AT = 102 * KB
 PAGE_AT = 110 * KB
+SCALES_AT = 134 * KB
 
 
 def tile_list_woven_video_residual_kernel(
@@ -66,8 +67,13 @@ def tile_list_woven_video_residual_kernel(
         def load_scale_rows(queue, dst, src):
             passes = src.shape[0]
             for q in range(QUADRANTS):
-                scale_rows = src[:, 4 * q : 4 * q + 4, :] if passes > 1 else src[0, 4 * q : 4 * q + 4, :]
-                queue.dma_start(dst[32 * q : 32 * q + 4 * passes, :].bitcast(I32), scale_rows.bitcast(I32))
+                queue.dma_start(
+                    dst[32 * q : 32 * q + 4 * passes, :].bitcast(I32), src[:, 4 * q : 4 * q + 4, :].bitcast(I32)
+                )
+
+        def load_scale_plane(dst, src):
+            for r in range(4):
+                nc.sync.dma_start(dst[r:P:32, :].bitcast(I32), src[0, r:16:4, :].bitcast(I32))
 
         def load_words(name, src, offset):
             words = placed(name, [P, T], U32, offset)
@@ -99,19 +105,19 @@ def tile_list_woven_video_residual_kernel(
         gate2 = {}
         idx = load_list("idx", offs)
         idx2 = load_list("idx2", offs2)
-        nc.sync.dma_start(w2_raw[:].bitcast(I32), w2_words[0].bitcast(I32))
-        load_scale_rows(nc.sync, tab_s, tab_scales)
-        tab_w = load_words("tab_w", tab_words[0], UP_AT)
-        load_scale_rows(nc.sync, tab2_s, tab2_scales)
-        w1_raw = [load_rows("w1_raw0", w1[:, 0:BANK], WOVEN_AT[0])]
-        load_scale_rows(nc.sync, w2_s_raw, w2_scales)
-        tab2_w = [load_words("tab2_w0", tab2_words[0], UP_AT + 8 * KB)]
         idx3 = load_list("idx3", offs3)
+        load_scale_plane(tab_s, tab_scales)
+        tab_w = load_words("tab_w", tab_words[0], SCALES_AT)
+        load_scale_rows(nc.gpsimd, tab2_s, tab2_scales)
+        load_scale_rows(nc.gpsimd, w3_s_raw, w3_scales)
+        w1_raw = [load_rows("w1_raw0", w1[:, 0:BANK], WOVEN_AT[0])]
+        nc.sync.dma_start(w2_raw[:].bitcast(I32), w2_words[0].bitcast(I32))
+        load_scale_plane(w2_s_raw, w2_scales)
+        tab2_w = [load_words("tab2_w0", tab2_words[0], UP_AT + 8 * KB)]
         gate1[0] = load_gate("gate1", wg1, 0)
         tab2_w.append(load_words("tab2_w1", tab2_words[1], PAGE_AT))
         w3_raw = placed("w3_raw", [P, 2, H], U32, UP_AT + 24 * KB)
         nc.sync.dma_start(w3_raw[:].bitcast(I32), w3_words.rearrange("a p c i -> p a (c i)").bitcast(I32))
-        load_scale_rows(nc.sync, w3_s_raw, w3_scales)
         gate1[1] = load_gate("gate1", wg1, 1)
         idx4 = load_list("idx4", offs4)
         gate2[0] = load_gate("gate2", wg2, 0)
@@ -129,13 +135,14 @@ def tile_list_woven_video_residual_kernel(
 
         v_s = kept("v_s", [P, S], U8)
         v_w = kept("v_w", [P, S], U32)
-        v2_s = kept("v2_s", [P, S], U8)
+        v2_s = placed("v2_s", [P, S], U8, SCALES_AT)
         first_sums = placed("first_sums", [P, S], F32, V2_AT + 4 * KB)
         v2_w = [placed("v2_w%d" % a, [P, S], U32, V2_AT + 4 * KB * a) for a in range(2)]
         w2_c = placed("w2_c", [P, 2 * H], U8, W2_AT)
         w2_s = kept("w2_s", [P, H], U8)
         w3_c = placed("w3_c", [P, 2, H], U32, W3_AT)
-        w3_s = kept("w3_s", [P, H], U8)
+        second_sums = placed("second_sums", [P, S], F32, SCALES_AT + 8 * KB)
+        w3_s = placed("w3_s", [P, H], U8, SCALES_AT + 8 * KB)
         first_squares = placed("first_squares", [P, S], F32, WOVEN_AT[1] + 4 * KB)
         w1_dealt = [placed("w1_dealt%d" % g, [P, BANK * PACK], BF16, WOVEN_AT[1] + 4 * KB * g) for g in range(2)]
         w1_c = {}
@@ -158,7 +165,7 @@ def tile_list_woven_video_residual_kernel(
             return first_lesser[i] if i < 2 else lesser[i % 2]
 
         def w1_sums(i):
-            return {0: first_sums, 1: lesser[1]}.get(i, h1_of(i - 1))
+            return {0: first_sums, 1: second_sums}.get(i, h1_of(i - 1))
 
         def gated_h1(i):
             return first_gated[i] if i < 2 else factor[i % 2]
@@ -297,8 +304,8 @@ def tile_list_woven_video_residual_kernel(
 
         nc.vector.tensor_copy(v_s[:], tab_s[:].indirect(idx[:]))
         nc.vector.tensor_copy(v_w[:], tab_w[:].indirect(idx[:]))
-        deal_pairs(w2_c[:], w2_raw[:], U32)
         deal_w1(0)
+        deal_pairs(w2_c[:], w2_raw[:], U32)
         deal_pairs(w2_s[:], w2_s_raw[:], U16)
         w1_c[0] = kept("w1_c0", [P, BANK], U32)
         w1_s[0] = kept("w1_s0", [P, BANK], U8)
@@ -382,5 +389,5 @@ def tile_list_woven_video_residual_kernel(
                 quantize_y(c - Y_LAG)
         for c in range(len(pieces) - Y_LAG, len(pieces)):
             quantize_y(c)
-        for q in range(QUADRANTS):
-            nc.sync.dma_start(out_2[0, 4 * q : 4 * q + 4, :].bitcast(I32), y_s[32 * q : 32 * q + 4, :].bitcast(I32))
+        for r in range(4):
+            nc.sync.dma_start(out_2[0, r:16:4, :].bitcast(I32), y_s[r:P:32, :].bitcast(I32))

@@ -26,6 +26,8 @@ ROW_TILES = H // P
 LAST = ROW_TILES - 1
 WIDTHS = (256, 512, 512, 512, 256)
 Y_LAG = 3
+CHOSEN = 384
+FIRST_CHOSEN = 7
 KB = 1024
 
 UP_AT = 0
@@ -35,7 +37,9 @@ V2_AT = 80 * KB
 W3_AT = 88 * KB
 W2_AT = 96 * KB
 STATIC_AT = 98 * KB
-MOVING_AT = 102 * KB
+SPARE_AT = 102 * KB
+RING_AT = 142 * KB
+RING = 9 * KB + KB // 2
 PAGE_AT = 110 * KB
 SCALES_AT = 134 * KB
 
@@ -113,7 +117,7 @@ def tile_list_woven_video_residual_kernel(
         w1_raw = [load_rows("w1_raw0", w1[:, 0:BANK], WOVEN_AT[0])]
         nc.sync.dma_start(w2_raw[:].bitcast(I32), w2_words[0].bitcast(I32))
         load_scale_plane(w2_s_raw, w2_scales)
-        tab2_w = [load_words("tab2_w0", tab2_words[0], UP_AT + 8 * KB)]
+        tab2_w = [load_words("tab2_w0", tab2_words[0], RING_AT + 5 * KB)]
         gate1[0] = load_gate("gate1", wg1, 0)
         tab2_w.append(load_words("tab2_w1", tab2_words[1], PAGE_AT))
         w3_raw = placed("w3_raw", [P, 2, H], U32, UP_AT + 24 * KB)
@@ -141,8 +145,8 @@ def tile_list_woven_video_residual_kernel(
         w2_c = placed("w2_c", [P, 2 * H], U8, W2_AT)
         w2_s = kept("w2_s", [P, H], U8)
         w3_c = placed("w3_c", [P, 2, H], U32, W3_AT)
-        second_sums = placed("second_sums", [P, S], F32, SCALES_AT + 8 * KB)
-        w3_s = placed("w3_s", [P, H], U8, SCALES_AT + 8 * KB)
+        second_sums = placed("second_sums", [P, S], F32, SPARE_AT)
+        w3_s = placed("w3_s", [P, H], U8, SPARE_AT)
         first_squares = placed("first_squares", [P, S], F32, WOVEN_AT[1] + 4 * KB)
         w1_dealt = [placed("w1_dealt%d" % g, [P, BANK * PACK], BF16, WOVEN_AT[1] + 4 * KB * g) for g in range(2)]
         w1_c = {}
@@ -151,21 +155,20 @@ def tile_list_woven_video_residual_kernel(
         w4_c = kept("w4_c", [P, 2, N], U32)
         y_c = kept("y_c", [P, T2], U32)
         y_s = kept("y_s", [P, T2], U8)
-        lesser = [kept("lesser%d" % k, [P, S], F32) for k in range(2)]
         factor = [kept("factor%d" % k, [P, S], F32) for k in range(2)]
         first_gated = [placed("first_gated0", [P, S], F32, PAIRS_AT), placed("first_gated1", [P, S], F32, STATIC_AT)]
-        moving = [placed("moving%d" % k, [P, S], F32, MOVING_AT + 4 * KB * k) for k in range(2)]
-
-        first_lesser = [placed("first_lesser%d" % k, [P, S], F32, UP_AT + 8 * KB + 4 * KB * k) for k in range(2)]
+        b = placed("b", [P, S], F32, SPARE_AT + 4 * KB)
+        signs = placed("signs", [P, CHOSEN], F32, STATIC_AT + 2 * KB + BANK)
+        choice = kept("choice", [P, 2 * CHOSEN], F32)
+        h1 = {}
+        gated_h2 = {}
+        sums = {0: first_sums, 1: second_sums}
 
         def first_bank(i):
             return PACK if i == 1 else 0
 
-        def h1_of(i):
-            return first_lesser[i] if i < 2 else lesser[i % 2]
-
-        def w1_sums(i):
-            return {0: first_sums, 1: second_sums}.get(i, h1_of(i - 1))
+        def chosen(i):
+            return CHOSEN if i >= FIRST_CHOSEN else 0
 
         def gated_h1(i):
             return first_gated[i] if i < 2 else factor[i % 2]
@@ -205,14 +208,29 @@ def tile_list_woven_video_residual_kernel(
                     lhsT_scale=w2_s[:, P * i : P * (i + 1)],
                     rhs=v_w[:, cols].bitcast(FP8X4), rhs_scale=v_s[:, cols], start=True, stop=True,
                 )
+            if i >= 2:
+                sums[i] = placed("sums%d" % i, [P, chosen(i) + S], F32, RING_AT + RING * ((i - 1) % 2) + 4 * KB)
+            f = chosen(i)
             for h, cols in enumerate(halves):
-                nc.scalar.copy(w1_sums(i)[:, cols], banks[first + h][:])
+                nc.scalar.copy(sums[i][:, f + cols.start : f + cols.stop], banks[first + h][:])
+            if f > 0:
+                nc.scalar.copy(sums[i][:, 0:f], banks[first + 2][:, 0:f])
+                nc.gpsimd.tensor_tensor(signs[:], sums[i][:, f : 2 * f], sums[i][:, 0:f], ALU.subtract)
+                nc.scalar.activation(signs[:], signs[:], ACT.Sign)
+                nc.scalar.activation(choice[:, 0:f], signs[:], ACT.Copy, scale=0.5, bias=0.5)
+                nc.scalar.activation(choice[:, f : 2 * f], signs[:], ACT.Copy, scale=-0.5, bias=0.5)
 
         def static_values(i):
-            h1 = h1_of(i)
-            for h, cols in enumerate(halves):
-                nc.vector.tensor_tensor(h1[:, cols], banks[first_bank(i) + 2 + h][:], w1_sums(i)[:, cols], ALU.min)
-            nc.gpsimd.tensor_tensor(gated_h1(i)[:], h1[:], gate1[i % PACK][:], ALU.mult)
+            h1[i] = placed("h1_%d" % i, [P, S], F32, RING_AT + RING * (i % 2) + 3 * KB)
+            f = chosen(i)
+            if f > 0:
+                nc.gpsimd.tensor_tensor(sums[i][:, 0 : 2 * f], sums[i][:, 0 : 2 * f], choice[:], ALU.mult)
+                nc.gpsimd.tensor_tensor(h1[i][:, 0:f], sums[i][:, 0:f], sums[i][:, f : 2 * f], ALU.add)
+            for h, (lo, hi) in enumerate(((f, BANK), (BANK, S))):
+                nc.vector.tensor_tensor(
+                    h1[i][:, lo:hi], banks[first_bank(i) + 2 + h][:, lo - BANK * h :], sums[i][:, f + lo : f + hi], ALU.min
+                )
+            nc.gpsimd.tensor_tensor(gated_h1(i)[:], h1[i][:], gate1[i % PACK][:], ALU.mult)
 
         def static_scatter(i):
             page[i] = placed("page%d" % i, [P, T2], F32, PAGE_AT + 8 * KB * (i % 3))
@@ -220,8 +238,7 @@ def tile_list_woven_video_residual_kernel(
 
         def moving_values(i):
             rows = slice(P * i, P * (i + 1))
-            b = moving[i % 2]
-            damp = lesser[0] if i == LAST else factor[i % 2]
+            damp = factor[0 if i == LAST else i % 2]
             squares = first_squares if i == 0 else damp
             for h, cols in enumerate(halves):
                 for a in range(2):
@@ -237,10 +254,11 @@ def tile_list_woven_video_residual_kernel(
             for cols in halves:
                 nc.scalar.activation(damp[:, cols], squares[:, cols], ACT.Abs_reciprocal_sqrt, bias=1.0)
             nc.gpsimd.tensor_tensor(b[:], b[:], gate2[i % PACK][:], ALU.mult)
-            nc.gpsimd.tensor_tensor(b[:], b[:], damp[:], ALU.mult)
+            gated_h2[i] = placed("gated_h2_%d" % i, [P, S], F32, RING_AT + RING * ((i + 1) % 2))
+            nc.gpsimd.tensor_tensor(gated_h2[i][:], b[:], damp[:], ALU.mult)
 
         def moving_scatter(i):
-            nc.vector.tensor_copy(page[i][:].indirect(idx4[:]), moving[i % 2][:])
+            nc.vector.tensor_copy(page[i][:].indirect(idx4[:]), gated_h2[i][:])
 
         def round_piece(i, c):
             g, t = divmod(i, PACK)
@@ -360,7 +378,7 @@ def tile_list_woven_video_residual_kernel(
             round_piece(LAST - 1, c)
         moving_scatter(LAST)
 
-        last_at = MOVING_AT + 4 * KB * (LAST % 2)
+        last_at = RING_AT + RING * ((LAST + 1) % 2)
         w4_s = placed("w4_s", [P, 2 * N], U8, last_at)
         z_c = [placed("z_c%d" % g, [P, T2], U32, at) for g, at in enumerate((W3_AT, V2_AT))]
         z_s = [placed("z_s%d" % g, [P, T2], U8, at) for g, at in enumerate((last_at + 2 * N, W2_AT))]

@@ -118,8 +118,8 @@ def tile_list_woven_video_residual_kernel(
         nc.sync.dma_start(w2_raw[:].bitcast(I32), w2_words[0].bitcast(I32))
         load_scale_plane(w2_s_raw, w2_scales)
         tab2_w = [load_words("tab2_w0", tab2_words[0], RING_AT + 5 * KB)]
+        tab2_w.append(load_words("tab2_w1", tab2_words[1], UP_AT + 16 * KB))
         gate1[0] = load_gate("gate1", wg1, 0)
-        tab2_w.append(load_words("tab2_w1", tab2_words[1], PAGE_AT))
         w3_raw = placed("w3_raw", [P, 2, H], U32, UP_AT + 24 * KB)
         nc.sync.dma_start(w3_raw[:].bitcast(I32), w3_words.rearrange("a p c i -> p a (c i)").bitcast(I32))
         gate1[1] = load_gate("gate1", wg1, 1)
@@ -354,8 +354,8 @@ def tile_list_woven_video_residual_kernel(
         for i in range(1, ROW_TILES):
             static_scatter(i)
             if i == 1:
-                w1_c[1] = placed("w1_c1", [P, BANK], U32, STATIC_AT)
-                w1_s[1] = placed("w1_s1", [P, BANK], U8, STATIC_AT + 2 * KB)
+                w1_c[1] = placed("w1_c1", [P, BANK], U32, SCALES_AT + 2 * KB)
+                w1_s[1] = placed("w1_s1", [P, BANK], U8, SCALES_AT + 4 * KB)
                 quantize_w1(1)
             if i < LAST:
                 static_values(i + 1)

@@ -25,7 +25,7 @@ LINE = 4
 ROW_TILES = H // P
 LAST = ROW_TILES - 1
 WIDTHS = (256, 512, 512, 512, 256)
-Y_LAG = 3
+Y_LAG = 2
 CHOSEN = 384
 FIRST_CHOSEN = 7
 KB = 1024

from contextlib import ExitStack

import concourse.mybir as mybir

K, K2, T, S, H, N, T2 = 512, 1024, 2048, 1024, 1024, 512, 2048
FLOPS = 2 * S * H * (2 * K + K2) + 2 * H * N * T2

F32 = mybir.dt.float32
BF16 = mybir.dt.bfloat16
I32 = mybir.dt.int32
U32 = mybir.dt.uint32
U16 = mybir.dt.uint16
U8 = mybir.dt.uint8
FP8X4 = mybir.dt.float8_e4m3fn_x4
FP4X4 = mybir.dt.float4_e2m1fn_x4
ALU = mybir.AluOpType
ACT = mybir.ActivationFunctionType

P = 128
PACK = 4
BANK = 512
QUADRANTS = 4
BY_HALVES = (0, 2, 1, 3)
LINE = 4
ROW_TILES = H // P
LAST = ROW_TILES - 1
WIDTHS = (256, 512, 512, 512, 256)
Y_LAG = 2
CHOSEN = 384
FIRST_CHOSEN = 7
KB = 1024

UP_AT = 0
WOVEN_AT = (32 * KB, 48 * KB)
PAIRS_AT = 64 * KB
V2_AT = 80 * KB
W3_AT = 88 * KB
W2_AT = 96 * KB
STATIC_AT = 98 * KB
SPARE_AT = 102 * KB
RING_AT = 142 * KB
RING = 9 * KB + KB // 2
PAGE_AT = 110 * KB
SCALES_AT = 134 * KB


def tile_list_woven_video_residual_kernel(
    tc, tab_words, tab_scales, tab2_words, tab2_scales, offs, offs2, offs3, offs4, w1,
    w2_words, w2_scales, w3_words, w3_scales, wg1, wg2, gain, w4, up, out_0, out_1, out_2,
):
    nc = tc.nc
    halves = (slice(0, BANK), slice(BANK, S))
    cuts = [sum(WIDTHS[:c]) for c in range(len(WIDTHS) + 1)]
    pieces = [slice(lo, hi) for lo, hi in zip(cuts, cuts[1:])]
    with ExitStack() as ctx:
        keep = ctx.enter_context(tc.tile_pool(name="keep", bufs=1))
        shared = ctx.enter_context(tc.tile_pool(name="shared", bufs=1))
        psum = ctx.enter_context(tc.psum_pool(name="psum", bufs=1))

        def kept(name, shape, dtype):
            return keep.tile(shape, dtype, name=name, align_bytes=64)

        def placed(name, shape, dtype, offset):
            return shared.tile(shape, dtype, name=name, align_bytes=64, offset=offset)

        def load_list(name, src):
            offsets = keep.tile([P, S // 16], U16, name=name)
            nc.sync.dma_start(offsets[:], src)
            return offsets

        def load_scale_rows(queue, dst, src):
            passes = src.shape[0]
            for q in range(QUADRANTS):
                queue.dma_start(
                    dst[32 * q : 32 * q + 4 * passes, :].bitcast(I32), src[:, 4 * q : 4 * q + 4, :].bitcast(I32)
                )

        def load_scale_plane(dst, src):
            for r in range(4):
                nc.sync.dma_start(dst[r:P:32, :].bitcast(I32), src[0, r:16:4, :].bitcast(I32))

        def load_words(name, src, offset):
            words = placed(name, [P, T], U32, offset)
            nc.sync.dma_start(words[:].bitcast(I32), src.rearrange("p t i -> p (t i)").bitcast(I32))
            return words

        def load_rows(name, src, offset):
            raw = placed(name, [P, PACK, src.shape[1]], F32, offset)
            nc.sync.dma_start(raw[:], src.rearrange("(p j) c -> p j c", j=PACK))
            return raw

        def load_gate(name, src, t):
            by_slot = src.rearrange("(i t e) j -> t i e j", t=PACK, e=2)
            tile = kept("%s_%d" % (name, t), [P, S], F32)
            for q in BY_HALVES:
                nc.sync.dma_start(tile[32 * q : 32 * q + 32, :], by_slot[t])
            return tile

        small_at = WOVEN_AT[1] + 8 * KB
        w2_raw = placed("w2_raw", [P, 2 * H], U8, small_at)
        tab_s = placed("tab_s", [P, T], U8, small_at + 2 * KB)
        tab2_s = placed("tab2_s", [P, T], U8, small_at + 4 * KB)
        w2_s_raw = placed("w2_s_raw", [P, H], U8, small_at + 6 * KB)
        w3_s_raw = placed("w3_s_raw", [P, H], U8, small_at + 7 * KB)
        for scale_tile in (tab_s, tab2_s, w2_s_raw, w3_s_raw):
            nc.vector.memset(scale_tile[:].bitcast(I32), 0)

        gate1 = {}
        gate2 = {}
        idx = load_list("idx", offs)
        idx2 = load_list("idx2", offs2)
        idx3 = load_list("idx3", offs3)
        load_scale_plane(tab_s, tab_scales)
        tab_w = load_words("tab_w", tab_words[0], SCALES_AT)
        load_scale_rows(nc.gpsimd, tab2_s, tab2_scales)
        load_scale_rows(nc.gpsimd, w3_s_raw, w3_scales)
        w1_raw = [load_rows("w1_raw0", w1[:, 0:BANK], WOVEN_AT[0])]
        nc.sync.dma_start(w2_raw[:].bitcast(I32), w2_words[0].bitcast(I32))
        load_scale_plane(w2_s_raw, w2_scales)
        tab2_w = [load_words("tab2_w0", tab2_words[0], RING_AT + 5 * KB)]
        tab2_w.append(load_words("tab2_w1", tab2_words[1], UP_AT + 16 * KB))
        gate1[0] = load_gate("gate1", wg1, 0)
        w3_raw = placed("w3_raw", [P, 2, H], U32, UP_AT + 24 * KB)
        nc.sync.dma_start(w3_raw[:].bitcast(I32), w3_words.rearrange("a p c i -> p a (c i)").bitcast(I32))
        gate1[1] = load_gate("gate1", wg1, 1)
        idx4 = load_list("idx4", offs4)
        gate2[0] = load_gate("gate2", wg2, 0)
        w1_raw.append(load_rows("w1_raw1", w1[:, BANK : 2 * BANK], WOVEN_AT[0] + 8 * KB))
        gate1[2] = load_gate("gate1", wg1, 2)
        gains = [kept("gains%d" % g, [P, PACK], F32) for g in range(2)]
        with nc.allow_non_contiguous_dma(reason="the four gains of a partition lie two elements apart"):
            for g in range(2):
                for e in range(2):
                    nc.sync.dma_start(gains[g][e:P:2, :], gain.rearrange("(g i t e) -> g e i t", g=2, t=PACK, e=2)[g, e])
        gate2[1] = load_gate("gate2", wg2, 1)
        gate1[3] = load_gate("gate1", wg1, 3)
        gate2[2] = load_gate("gate2", wg2, 2)
        gate2[3] = load_gate("gate2", wg2, 3)

        v_s = kept("v_s", [P, S], U8)
        v_w = kept("v_w", [P, S], U32)
        v2_s = placed("v2_s", [P, S], U8, SCALES_AT)
        first_sums = placed("first_sums", [P, S], F32, V2_AT + 4 * KB)
        v2_w = [placed("v2_w%d" % a, [P, S], U32, V2_AT + 4 * KB * a) for a in range(2)]
        w2_c = placed("w2_c", [P, 2 * H], U8, W2_AT)
        w2_s = kept("w2_s", [P, H], U8)
        w3_c = placed("w3_c", [P, 2, H], U32, W3_AT)
        second_sums = placed("second_sums", [P, S], F32, SPARE_AT)
        w3_s = placed("w3_s", [P, H], U8, SPARE_AT)
        first_squares = placed("first_squares", [P, S], F32, WOVEN_AT[1] + 4 * KB)
        w1_dealt = [placed("w1_dealt%d" % g, [P, BANK * PACK], BF16, WOVEN_AT[1] + 4 * KB * g) for g in range(2)]
        w1_c = {}
        w1_s = {}
        w4_dealt = kept("w4_dealt", [P, 2, N * PACK], BF16)
        w4_c = kept("w4_c", [P, 2, N], U32)
        y_c = kept("y_c", [P, T2], U32)
        y_s = kept("y_s", [P, T2], U8)
        factor = [kept("factor%d" % k, [P, S], F32) for k in range(2)]
        first_gated = [placed("first_gated0", [P, S], F32, PAIRS_AT), placed("first_gated1", [P, S], F32, STATIC_AT)]
        b = placed("b", [P, S], F32, SPARE_AT + 4 * KB)
        signs = placed("signs", [P, CHOSEN], F32, STATIC_AT + 2 * KB + BANK)
        choice = kept("choice", [P, 2 * CHOSEN], F32)
        h1 = {}
        gated_h2 = {}
        sums = {0: first_sums, 1: second_sums}

        def first_bank(i):
            return PACK if i == 1 else 0

        def chosen(i):
            return CHOSEN if i >= FIRST_CHOSEN else 0

        def gated_h1(i):
            return first_gated[i] if i < 2 else factor[i % 2]
        banks = [psum.tile([P, BANK], F32, name="bank%d" % k) for k in range(2 * PACK)]
        page = {}
        pairs = {}
        z_woven = {}
        y_woven = {}

        def deal_pairs(dst, src, dtype):
            nc.scalar.copy(
                dst.bitcast(dtype).rearrange("p (g t i) -> p g i t", g=2, t=PACK),
                src.bitcast(dtype).rearrange("p (g i t) -> p g i t", g=2, t=PACK),
            )

        def deal_w1(g):
            nc.scalar.copy(
                w1_dealt[g][:].rearrange("p (t i e j) -> p i t j e", t=PACK, e=2, j=PACK),
                w1_raw[g][:].rearrange("p j (i t e) -> p i t j e", t=PACK, e=2),
            )

        def quantize_w1(g):
            nc.vector.quantize_mx(out=w1_c[g][:].bitcast(FP8X4), scales=w1_s[g][:], in_=w1_dealt[g][:])

        def static_products(i):
            g, t = divmod(i, PACK)
            first = first_bank(i)
            for h, cols in enumerate(halves):
                nc.tensor.matmul_mx(
                    out=banks[first + h][:], lhsT=w1_c[g][:, P * t : P * (t + 1)].bitcast(FP8X4),
                    lhsT_scale=w1_s[g][:, P * t : P * (t + 1)],
                    rhs=v_w[:, cols].bitcast(FP8X4), rhs_scale=v_s[:, cols], start=True, stop=True,
                )
            for h, cols in enumerate(halves):
                nc.tensor.matmul_mx(
                    out=banks[first + 2 + h][:], lhsT=w2_c[:, 2 * P * i : 2 * P * (i + 1)].bitcast(FP4X4),
                    lhsT_scale=w2_s[:, P * i : P * (i + 1)],
                    rhs=v_w[:, cols].bitcast(FP8X4), rhs_scale=v_s[:, cols], start=True, stop=True,
                )
            if i >= 2:
                sums[i] = placed("sums%d" % i, [P, chosen(i) + S], F32, RING_AT + RING * ((i - 1) % 2) + 4 * KB)
            f = chosen(i)
            for h, cols in enumerate(halves):
                nc.scalar.copy(sums[i][:, f + cols.start : f + cols.stop], banks[first + h][:])
            if f > 0:
                nc.scalar.copy(sums[i][:, 0:f], banks[first + 2][:, 0:f])
                nc.gpsimd.tensor_tensor(signs[:], sums[i][:, f : 2 * f], sums[i][:, 0:f], ALU.subtract)
                nc.scalar.activation(signs[:], signs[:], ACT.Sign)
                nc.scalar.activation(choice[:, 0:f], signs[:], ACT.Copy, scale=0.5, bias=0.5)
                nc.scalar.activation(choice[:, f : 2 * f], signs[:], ACT.Copy, scale=-0.5, bias=0.5)

        def static_values(i):
            h1[i] = placed("h1_%d" % i, [P, S], F32, RING_AT + RING * (i % 2) + 3 * KB)
            f = chosen(i)
            if f > 0:
                nc.gpsimd.tensor_tensor(sums[i][:, 0 : 2 * f], sums[i][:, 0 : 2 * f], choice[:], ALU.mult)
                nc.gpsimd.tensor_tensor(h1[i][:, 0:f], sums[i][:, 0:f], sums[i][:, f : 2 * f], ALU.add)
            for h, (lo, hi) in enumerate(((f, BANK), (BANK, S))):
                nc.vector.tensor_tensor(
                    h1[i][:, lo:hi], banks[first_bank(i) + 2 + h][:, lo - BANK * h :], sums[i][:, f + lo : f + hi], ALU.min
                )
            nc.gpsimd.tensor_tensor(gated_h1(i)[:], h1[i][:], gate1[i % PACK][:], ALU.mult)

        def static_scatter(i):
            page[i] = placed("page%d" % i, [P, T2], F32, PAGE_AT + 8 * KB * (i % 3))
            nc.vector.tensor_copy(page[i][:].indirect(idx3[:]), gated_h1(i)[:])

        def moving_values(i):
            rows = slice(P * i, P * (i + 1))
            damp = factor[0 if i == LAST else i % 2]
            squares = first_squares if i == 0 else damp
            for h, cols in enumerate(halves):
                for a in range(2):
                    nc.tensor.matmul_mx(
                        out=banks[4 + h][:], lhsT=w3_c[:, a, rows].bitcast(FP8X4), lhsT_scale=w3_s[4 * a :, rows],
                        rhs=v2_w[a][:, cols].bitcast(FP8X4), rhs_scale=v2_s[4 * a :, cols],
                        start=(a == 0), stop=(a == 1),
                    )
            for h, cols in enumerate(halves):
                nc.scalar.copy(b[:, cols], banks[4 + h][:])
            for h, cols in enumerate(halves):
                nc.scalar.activation(squares[:, cols], banks[4 + h][:], ACT.Square)
            for cols in halves:
                nc.scalar.activation(damp[:, cols], squares[:, cols], ACT.Abs_reciprocal_sqrt, bias=1.0)
            nc.gpsimd.tensor_tensor(b[:], b[:], gate2[i % PACK][:], ALU.mult)
            gated_h2[i] = placed("gated_h2_%d" % i, [P, S], F32, RING_AT + RING * ((i + 1) % 2))
            nc.gpsimd.tensor_tensor(gated_h2[i][:], b[:], damp[:], ALU.mult)

        def moving_scatter(i):
            nc.vector.tensor_copy(page[i][:].indirect(idx4[:]), gated_h2[i][:])

        def round_piece(i, c):
            g, t = divmod(i, PACK)
            cols = pieces[c]
            if t == 0:
                pairs[g, c] = placed("pairs%d_%d" % (g, c), [P, 2, WIDTHS[c], 2], BF16, PAIRS_AT + 8 * cols.start)
            nc.scalar.activation(
                pairs[g, c][:, t // 2, :, t % 2], page[i][:, cols], ACT.Copy, scale=gains[g][:, t : t + 1]
            )

        def weave_piece(g, c):
            cols = pieces[c]
            z_woven[g, c] = placed("z_woven%d_%d" % (g, c), [P, WIDTHS[c] * PACK], BF16, WOVEN_AT[g] + 8 * cols.start)
            nc.scalar.copy(
                z_woven[g, c][:].bitcast(U32).rearrange("p (m u) -> p m u", u=2),
                pairs[g, c][:].rearrange("p u m e -> p (u m e)").bitcast(U32).rearrange("p (u m) -> p m u", u=2),
            )

        def deal_w4(g):
            nc.scalar.copy(
                w4_dealt[:, g, :].rearrange("p (t m j) -> p m t j", t=PACK, j=PACK),
                w4_raw[g][:].rearrange("p j (m t) -> p m t j", t=PACK),
            )

        def quantize_z(g, c):
            cols = pieces[c]
            nc.vector.quantize_mx(out=z_c[g][:, cols].bitcast(FP8X4), scales=z_s[g][:, cols], in_=z_woven[g, c][:])

        def y_bank(c, t):
            return banks[PACK * ((c + 1) % 2) + t][:, 0 : WIDTHS[c]]

        def project(c):
            cols = pieces[c]
            for g in range(2):
                for t in range(PACK):
                    nc.tensor.matmul_mx(
                        out=y_bank(c, t), lhsT=w4_c[:, g, P * t : P * (t + 1)].bitcast(FP8X4),
                        lhsT_scale=w4_s[:, N * g + P * t : N * g + P * (t + 1)],
                        rhs=z_c[g][:, cols].bitcast(FP8X4), rhs_scale=z_s[g][:, cols], start=(g == 0), stop=(g == 1),
                    )

        out_rows = out_0.rearrange("(p t) c -> p t c", t=PACK)
        out_words = out_1[0].rearrange("p m t -> p (m t)").bitcast(I32)

        def add_up(c):
            cols = pieces[c]
            for t in range(PACK):
                nc.vector.tensor_tensor(y[c][:, t, :], y_bank(c, t), y[c][:, t, :], ALU.add)
                if t % 2 == 1:
                    nc.sync.dma_start(out_rows[:, t - 1 : t + 1, cols], y[c][:, t - 1 : t + 1, :])
            y_woven[c] = placed("y_woven%d" % c, [P, WIDTHS[c] * PACK], BF16, WOVEN_AT[0] + 8 * cols.start)
            nc.scalar.copy(
                y_woven[c][:].rearrange("p (m e t) -> p m t e", e=LINE, t=PACK),
                y[c][:].rearrange("p t (m e) -> p m t e", e=LINE),
            )

        def quantize_y(c):
            cols = pieces[c]
            nc.vector.quantize_mx(out=y_c[:, cols].bitcast(FP8X4), scales=y_s[:, cols], in_=y_woven[c][:])
            nc.sync.dma_start(out_words[:, cols], y_c[:, cols].bitcast(I32))

        nc.vector.tensor_copy(v_s[:], tab_s[:].indirect(idx[:]))
        nc.vector.tensor_copy(v_w[:], tab_w[:].indirect(idx[:]))
        deal_w1(0)
        deal_pairs(w2_c[:], w2_raw[:], U32)
        deal_pairs(w2_s[:], w2_s_raw[:], U16)
        w1_c[0] = kept("w1_c0", [P, BANK], U32)
        w1_s[0] = kept("w1_s0", [P, BANK], U8)
        quantize_w1(0)
        nc.vector.tensor_copy(v2_s[:], tab2_s[:].indirect(idx2[:]))
        static_products(0)
        nc.vector.tensor_copy(v2_w[0][:], tab2_w[0][:].indirect(idx2[:]))
        static_values(0)
        static_products(1)
        nc.vector.tensor_copy(v2_w[1][:], tab2_w[1][:].indirect(idx2[:]))
        static_values(1)
        nc.scalar.copy(
            w3_c[:].rearrange("p a c -> p (a c)").rearrange("p (u t i e) -> p u i t e", u=4, t=PACK, e=2),
            w3_raw[:].rearrange("p a c -> p (a c)").rearrange("p (u i t e) -> p u i t e", u=4, t=PACK, e=2),
        )
        deal_pairs(w3_s[:], w3_s_raw[:], U16)
        static_scatter(0)
        moving_values(0)
        deal_w1(1)
        static_products(2)
        w4_raw = [placed("w4_raw%d" % g, [P, PACK, N], F32, WOVEN_AT[1] + 8 * KB * (1 - g)) for g in range(2)]
        w4_rows = w4.rearrange("(g i t e) n -> g t i e n", g=2, t=PACK, e=2)
        for g in range(2):
            for t in range(PACK):
                nc.sync.dma_start(w4_raw[g][:, t, :], w4_rows[g, t])
        y = [load_rows("y%d" % c, up[:, cols], UP_AT + 16 * cols.start) for c, cols in enumerate(pieces)]

        for i in range(1, ROW_TILES):
            static_scatter(i)
            if i == 1:
                w1_c[1] = placed("w1_c1", [P, BANK], U32, SCALES_AT + 2 * KB)
                w1_s[1] = placed("w1_s1", [P, BANK], U8, SCALES_AT + 4 * KB)
                quantize_w1(1)
            if i < LAST:
                static_values(i + 1)
            if i == LAST:
                moving_values(LAST)
            if i >= 2:
                for c in range(len(pieces)):
                    round_piece(i - 2, c)
            if i < LAST:
                moving_values(i)
            moving_scatter(i - 1)
            if i + 2 <= LAST:
                static_products(i + 2)
            if i in (2, 3):
                deal_w4(i - 2)
            if i - 2 == PACK - 1:
                for c in range(len(pieces)):
                    weave_piece(0, c)
        for c in range(len(pieces)):
            round_piece(LAST - 1, c)
        moving_scatter(LAST)

        last_at = RING_AT + RING * ((LAST + 1) % 2)
        w4_s = placed("w4_s", [P, 2 * N], U8, last_at)
        z_c = [placed("z_c%d" % g, [P, T2], U32, at) for g, at in enumerate((W3_AT, V2_AT))]
        z_s = [placed("z_s%d" % g, [P, T2], U8, at) for g, at in enumerate((last_at + 2 * N, W2_AT))]
        nc.vector.quantize_mx(
            out=w4_c[:].rearrange("p g n -> p (g n)").bitcast(FP8X4), scales=w4_s[:],
            in_=w4_dealt[:].rearrange("p g n -> p (g n)"),
        )
        for c in range(len(pieces)):
            round_piece(LAST, c)
            weave_piece(1, c)
        quantize_z(0, 0)
        quantize_z(1, 0)
        project(0)
        quantize_z(0, 1)
        quantize_z(0, 2)
        quantize_z(1, 1)
        project(1)
        quantize_z(0, 3)
        quantize_z(0, 4)
        for c in range(len(pieces)):
            add_up(c)
            if c + 2 < len(pieces):
                quantize_z(1, c + 2)
                project(c + 2)
            if c >= Y_LAG:
                quantize_y(c - Y_LAG)
        for c in range(len(pieces) - Y_LAG, len(pieces)):
            quantize_y(c)
        for r in range(4):
            nc.sync.dma_start(out_2[0, r:16:4, :].bitcast(I32), y_s[r:P:32, :].bitcast(I32))
